import numpy as np
import ml_dtypes


def mxq(x, axis, fmt="e4m3"):
    dtype, down = {"e4m3": (ml_dtypes.float8_e4m3fn, 7), "e5m2": (ml_dtypes.float8_e5m2, 14)}[fmt]
    v = np.moveaxis(np.asarray(x, np.float32).astype(ml_dtypes.bfloat16).astype(np.float64), axis, -1)
    blocks = v.reshape(v.shape[:-1] + (-1, 32))
    amax = np.abs(blocks).max(-1, keepdims=True)
    byte = np.maximum(np.where(amax > 0, np.frexp(amax)[1] - 1 + 127, 0) - down, 1)
    scale = np.exp2(byte - 127.0)
    codes = (blocks / scale).astype(np.float32).astype(dtype).astype(np.float64)
    return np.moveaxis((codes * scale).reshape(v.shape), -1, axis)


WIDE = False


def mx_kscale(k):
    if not WIDE:
        return np.ones(k)
    levels = np.array([10, -10, 5, -5, 0])
    if k % 512:
        return np.exp2(np.random.permutation(np.resize(levels, k // 32))).repeat(32)
    a = np.empty((k // 512, 16))
    for p in range(k // 512):
        a[p, :8] = np.random.permutation(np.resize(levels, 8))
        for g in range(8):
            far = levels[np.abs(levels - a[p, g]) >= 10]
            a[p, g + 8] = far[np.random.randint(len(far))]
    return np.exp2(a.ravel()).repeat(32)


def f64(x):
    return np.asarray(x).astype(np.float64)


def striped(idx):
    return np.tile(idx.reshape(-1, 16).T, (8, 1)).astype(np.uint16)


def unstriped(offs):
    return offs[:16].T.reshape(-1).astype(np.int64)


E2M1 = np.array([0.0, 0.5, 1.0, 1.5, 2.0, 3.0, 4.0, 6.0, -0.0, -0.5, -1.0, -1.5, -2.0, -3.0, -4.0, -6.0])


def pack_weight(w, fmt):
    k, n = w.shape
    w = f64(np.asarray(w, np.float32).astype(ml_dtypes.bfloat16)).reshape(k // 32, 32, n)
    amax = np.abs(w).max(1)
    if fmt == "e4m3":
        byte = np.frexp(amax)[1] - 1 + 127 - 7
    else:
        mant, ex = np.frexp(amax / 6.0)
        byte = np.where(mant > 0.5, ex, ex - 1) + 127
    byte = np.clip(np.where(amax > 0, byte, 1), 1, 254)
    scaled = (w * np.exp2(127.0 - byte)[:, None, :]).reshape(k, n).astype(np.float32)
    by_word = np.ascontiguousarray(scaled.reshape(k // 512, 128, 4, n).transpose(0, 1, 3, 2))
    if fmt == "e4m3":
        words = by_word.astype(ml_dtypes.float8_e4m3fn).view(np.uint8)
    else:
        c = by_word.astype(ml_dtypes.float4_e2m1fn).view(np.uint8) & 0xF
        words = (c[..., 0::2] | (c[..., 1::2] << 4)).reshape(k // 512, 128, 2 * n)
    return np.ascontiguousarray(words), np.ascontiguousarray(byte.astype(np.uint8).reshape(k // 512, 16, n))


def unpack_weight(words, scales, fmt):
    g, _, n = scales.shape
    words = np.ascontiguousarray(words).reshape(g, 128, n, -1)
    if fmt == "e4m3":
        vals = words.view(ml_dtypes.float8_e4m3fn).astype(np.float64)
    else:
        nib = np.empty((g, 128, n, 4), np.uint8)
        nib[..., 0::2] = words & 0xF
        nib[..., 1::2] = words >> 4
        vals = E2M1[nib]
    vals = vals * np.repeat(np.exp2(scales.astype(np.float64) - 127.0), 8, axis=1)[..., None]
    return vals.transpose(0, 1, 3, 2).reshape(g * 512, n)


def gelu(v):
    return 0.5 * v * (1.0 + np.tanh(np.sqrt(2.0 / np.pi) * (v + 0.044715 * v**3)))


K, T, S, T2, S2, N = 1536, 2048, 1024, 1024, 512, 768

def setup_inputs():
    n = np.random.standard_normal
    s = mx_kscale(K)[:, None]
    u = mx_kscale(S)[:, None]
    tab_words, tab_scales = pack_weight(n((K, T)) * s, "e4m3")
    tab2_words, tab2_scales = pack_weight(n((K, T2)) / np.sqrt(K) / s, "e4m3")
    m4_words, m4_scales = pack_weight(1.2 * n((S, N)) / np.sqrt(S) / u, "e2m1")
    edges = np.random.random((S, S2)) < 0.5
    return {
        "tab_words": tab_words, "tab_scales": tab_scales,
        "tab2_words": tab2_words, "tab2_scales": tab2_scales,
        "offs": striped(np.random.permutation(T)[:S]),
        "offs2": striped(np.random.permutation(T2)[:S2]),
        "adj": (np.exp(0.3 * n((S, S2))) * edges).astype(np.float32),
        "deg": (np.exp(0.3 * n(S)) * u[:, 0]).astype(np.float32),
        "m4_words": m4_words, "m4_scales": m4_scales,
        "wg": (1.2 * n((S, N)) / np.sqrt(S) / u).astype(np.float32),
        "bg": (0.5 * n(N)).astype(np.float32),
    }

def reference(tab_words, tab_scales, tab2_words, tab2_scales, offs, offs2, adj, deg,
              m4_words, m4_scales, wg, bg):
    v = unpack_weight(tab_words, tab_scales, "e4m3")[:, unstriped(offs)]
    v2 = unpack_weight(tab2_words, tab2_scales, "e4m3")[:, unstriped(offs2)]
    a = v.T @ v2
    h = a * f64(adj) * f64(deg)[:, None]
    hq = mxq(h, 0, "e4m3")
    m4 = unpack_weight(m4_words, m4_scales, "e2m1")
    y = m4.T @ hq
    g = mxq(f64(wg), 0, "e4m3").T @ hq
    gate = 1.0 / (1.0 + np.exp(-(g + f64(bg)[:, None])))
    return y * gate

@@ -1,0 +1,228 @@
+from contextlib import ExitStack
+
+import concourse.mybir as mybir
+
+K, T, S, T2, S2, N = 1536, 2048, 1024, 1024, 512, 768
+FLOPS = 2 * K * S * S2 + 2 * 2 * S * N * S2
+
+F32 = mybir.dt.float32
+BF16 = mybir.dt.bfloat16
+I32 = mybir.dt.int32
+U32 = mybir.dt.uint32
+U16 = mybir.dt.uint16
+U8 = mybir.dt.uint8
+FP8X4 = mybir.dt.float8_e4m3fn_x4
+FP4X4 = mybir.dt.float4_e2m1fn_x4
+MULT = mybir.AluOpType.mult
+COPY = mybir.ActivationFunctionType.Copy
+SIGMOID = mybir.ActivationFunctionType.Sigmoid
+
+P = 128
+PACK = 4
+PASS = P * PACK
+K_PASSES = K // PASS
+I_PASSES = S // PASS
+QUADRANTS = 4
+SCALE_ROWS = 4
+J_CHUNK = 128
+J_CHUNKS = S2 // J_CHUNK
+W_CHUNK = 256
+W_CHUNKS = N // W_CHUNK
+N_TILES = N // P
+BANKS = 8
+LIST_COLS = PASS // 16
+RUN = 4
+
+
+def tile_list_gated_graph_messages_kernel(
+    tc, tab_words, tab_scales, tab2_words, tab2_scales, offs, offs2, adj, deg, m4_words, m4_scales, wg, bg, out
+):
+    nc = tc.nc
+    with ExitStack() as ctx:
+        lists = ctx.enter_context(tc.tile_pool(name="lists", bufs=1))
+        keep = ctx.enter_context(tc.tile_pool(name="keep", bufs=1))
+        psum = ctx.enter_context(tc.psum_pool(name="psum", bufs=1))
+
+        def sbuf(name, shape, dtype):
+            return keep.tile(shape, dtype, name=name, align_bytes=64)
+
+        def bank(index, shape):
+            return psum.tile(shape, F32, name="bank", tag="bank%d" % index)
+
+        centre_scales = sbuf("centre_scales", [P, T2], U8)
+        neigh_scales = sbuf("neigh_scales", [P, T], U8)
+        msg_scales = sbuf("msg_scales", [P, I_PASSES, N], U8)
+        nc.vector.memset(centre_scales[:].bitcast(I32), 0)
+        nc.vector.memset(neigh_scales[:].bitcast(I32), 0)
+        nc.vector.memset(msg_scales[:].bitcast(I32), 0)
+        for queue, tile, source in ((nc.scalar, centre_scales, tab2_scales), (nc.gpsimd, neigh_scales, tab_scales)):
+            for q in range(QUADRANTS):
+                queue.dma_start(
+                    out=tile[32 * q : 32 * q + SCALE_ROWS * K_PASSES, :].bitcast(I32),
+                    in_=source[:, SCALE_ROWS * q : SCALE_ROWS * (q + 1), :].bitcast(I32),
+                )
+        for q in range(QUADRANTS):
+            nc.gpsimd.dma_start(
+                out=msg_scales[32 * q : 32 * q + SCALE_ROWS, :, :].bitcast(I32),
+                in_=m4_scales[:, SCALE_ROWS * q : SCALE_ROWS * (q + 1), :].rearrange("a r n -> r a n").bitcast(I32),
+            )
+
+        def load_words(name, source, a):
+            words = sbuf("%s%d" % (name, a), [P, source.shape[2]], U32)
+            nc.sync.dma_start(out=words[:].bitcast(I32), in_=source[a].rearrange("p n t -> p (n t)").bitcast(I32))
+            return words
+
+        def load_adj(b):
+            rows = sbuf("adj%d" % b, [P, PACK, S2], F32)
+            nc.sync.dma_start(out=rows[:], in_=adj[b * PASS : (b + 1) * PASS, :].rearrange("(p t) j -> p t j", t=PACK))
+            return rows
+
+        def load_wg(b, c):
+            rows = sbuf("wg%d_%d" % (b, c), [P, PACK, W_CHUNK], F32)
+            source = wg[b * PASS : (b + 1) * PASS, c * W_CHUNK : (c + 1) * W_CHUNK]
+            nc.sync.dma_start(out=rows[:], in_=source.rearrange("(p t) n -> p t n", t=PACK))
+            return rows
+
+        centre_list = lists.tile([P, S2 // 16], U16, name="centre_list")
+        neigh_list = lists.tile([P, S // 16], U16, name="neigh_list")
+        nc.sync.dma_start(centre_list[:], offs2)
+        centre_table = [load_words("centre_table", tab2_words, a) for a in range(K_PASSES)]
+        nc.sync.dma_start(neigh_list[:], offs)
+        neigh_table = [load_words("neigh_table", tab_words, 0)]
+        deg_cols = sbuf("deg_cols", [P, I_PASSES, PACK], F32)
+        nc.sync.dma_start(out=deg_cols[:], in_=deg.rearrange("(b p t) -> p b t", p=P, t=PACK))
+        adj_rows = [load_adj(0)]
+        neigh_table.extend(load_words("neigh_table", tab_words, a) for a in range(1, K_PASSES))
+        adj_rows.append(load_adj(1))
+        wg_rows = {(0, c): load_wg(0, c) for c in range(W_CHUNKS)}
+        msg_words = sbuf("msg_words", [P, I_PASSES, 2 * N], U8)
+        nc.sync.dma_start(out=msg_words[:].bitcast(I32), in_=m4_words.rearrange("a p c -> p a c").bitcast(I32))
+        bias_cols = sbuf("bias_cols", [P, N_TILES], F32)
+        with nc.allow_non_contiguous_dma(reason="one bias value a partition"):
+            nc.sync.dma_start(out=bias_cols[:], in_=bg.rearrange("(n p) -> p n", p=P))
+        for c in range(W_CHUNKS):
+            wg_rows[(1, c)] = load_wg(1, c)
+
+        centre_words = []
+        for a in range(K_PASSES):
+            picked = sbuf("centre_words%d" % a, [P, S2], U32)
+            nc.vector.tensor_copy(picked[:], centre_table[a][:].indirect(centre_list[:]))
+            centre_words.append(picked)
+        centre_bytes = sbuf("centre_bytes", [P, S2], U8)
+        nc.vector.tensor_copy(centre_bytes[:], centre_scales[:].indirect(centre_list[:]))
+
+        def part_of_list(b):
+            return neigh_list[:, b * LIST_COLS : (b + 1) * LIST_COLS]
+
+        def gather_neigh_words(a, b):
+            picked = sbuf("neigh_words%d_%d" % (a, b), [P, PACK, P], U32)
+            nc.vector.tensor_copy(picked[:].rearrange("p t m -> p m t"), neigh_table[a][:].indirect(part_of_list(b)))
+            return picked
+
+        def gather_neigh_bytes(b):
+            picked = sbuf("neigh_picked%d" % b, [P, PASS], U8)
+            nc.vector.tensor_copy(picked[:], neigh_scales[:].indirect(part_of_list(b)))
+            return picked
+
+        def deal_neigh_bytes(b, picked):
+            dealt = sbuf("neigh_bytes%d" % b, [P, PACK, P], U8)
+            nc.vector.tensor_copy(dealt[:], picked[:].rearrange("p (m t) -> p t m", t=PACK))
+            return dealt
+
+        neigh_words = {(0, b): gather_neigh_words(0, b) for b in range(I_PASSES)}
+        picked_bytes = [gather_neigh_bytes(b) for b in range(I_PASSES)]
+        neigh_bytes = [deal_neigh_bytes(b, picked_bytes[b]) for b in range(I_PASSES)]
+
+        compare = {(b, c): bank(b * J_CHUNKS + c, [P, PACK, J_CHUNK]) for b in range(I_PASSES) for c in range(J_CHUNKS)}
+        for a in range(K_PASSES):
+            for b in range(I_PASSES):
+                if a > 0:
+                    neigh_words[(a, b)] = gather_neigh_words(a, b)
+                for c in range(J_CHUNKS):
+                    cols = slice(c * J_CHUNK, (c + 1) * J_CHUNK)
+                    for t in range(PACK):
+                        nc.tensor.matmul_mx(
+                            out=compare[(b, c)][:, t, :],
+                            lhsT=neigh_words[(a, b)][:, t, :].bitcast(FP8X4),
+                            lhsT_scale=neigh_bytes[b][SCALE_ROWS * a :, t, :],
+                            rhs=centre_words[a][:, cols].bitcast(FP8X4),
+                            rhs_scale=centre_bytes[SCALE_ROWS * a :, cols],
+                            start=(a == 0 and t == 0),
+                            stop=(a == K_PASSES - 1 and t == PACK - 1),
+                        )
+
+        h_codes, h_scales = [], []
+        for b in range(I_PASSES):
+            weight = sbuf("edge_weight%d" % b, [P, PACK, S2], F32)
+            for t in range(PACK):
+                nc.scalar.activation(weight[:, t, :], adj_rows[b][:, t, :], COPY, scale=deg_cols[:, b, t : t + 1])
+            h_bf16 = sbuf("h_bf16_%d" % b, [P, S2, PACK], BF16)
+            for c in range(J_CHUNKS):
+                cols = slice(c * J_CHUNK, (c + 1) * J_CHUNK)
+                nc.vector.tensor_tensor(
+                    h_bf16[:, cols, :].rearrange("p (r i) t -> p r t i", i=RUN),
+                    compare[(b, c)][:].rearrange("p t (r i) -> p r t i", i=RUN),
+                    weight[:, :, cols].rearrange("p t (r i) -> p r t i", i=RUN),
+                    MULT,
+                )
+            codes = sbuf("h_codes%d" % b, [P, S2], U32)
+            scales = sbuf("h_scales%d" % b, [P, S2], U8)
+            nc.vector.quantize_mx(out=codes[:].bitcast(FP8X4), scales=scales[:], in_=h_bf16[:].rearrange("p j t -> p (j t)"))
+            h_codes.append(codes)
+            h_scales.append(scales)
+
+        wg_codes, wg_scales = {}, {}
+        for b in range(I_PASSES):
+            for c in range(W_CHUNKS):
+                wg_bf16 = sbuf("wg_bf16_%d_%d" % (b, c), [P, W_CHUNK, PACK], BF16)
+                nc.scalar.copy(
+                    wg_bf16[:].rearrange("p (r i) t -> p r t i", i=RUN),
+                    wg_rows[(b, c)][:].rearrange("p t (r i) -> p r t i", i=RUN),
+                )
+                codes = sbuf("wg_codes%d_%d" % (b, c), [P, W_CHUNK], U32)
+                scales = sbuf("wg_scales%d_%d" % (b, c), [P, W_CHUNK], U8)
+                nc.vector.quantize_mx(out=codes[:].bitcast(FP8X4), scales=scales[:], in_=wg_bf16[:].rearrange("p n t -> p (n t)"))
+                wg_codes[(b, c)] = codes
+                wg_scales[(b, c)] = scales
+
+        def message_pass(n, b, acc):
+            nc.tensor.matmul_mx(
+                out=acc[:],
+                lhsT=msg_words[:, b, 2 * P * n : 2 * P * (n + 1)].bitcast(FP4X4),
+                lhsT_scale=msg_scales[:, b, P * n : P * (n + 1)],
+                rhs=h_codes[b][:].bitcast(FP8X4),
+                rhs_scale=h_scales[b][:],
+                start=(b == 0),
+                stop=(b == I_PASSES - 1),
+            )
+
+        def gate_pass(n, b, acc):
+            c, first = divmod(n * P, W_CHUNK)
+            nc.tensor.matmul_mx(
+                out=acc[:],
+                lhsT=wg_codes[(b, c)][:, first : first + P].bitcast(FP8X4),
+                lhsT_scale=wg_scales[(b, c)][:, first : first + P],
+                rhs=h_codes[b][:].bitcast(FP8X4),
+                rhs_scale=h_scales[b][:],
+                start=(b == 0),
+                stop=(b == I_PASSES - 1),
+            )
+
+        def finish(n, y_acc, g_acc):
+            gate = sbuf("gate%d" % n, [P, S2], F32)
+            nc.scalar.activation(gate[:], g_acc[:], SIGMOID, bias=bias_cols[:, n : n + 1])
+            result = sbuf("result%d" % n, [P, S2], F32)
+            nc.vector.tensor_tensor(result[:], y_acc[:], gate[:], MULT)
+            nc.sync.dma_start(out=out[n * P : (n + 1) * P, :], in_=result[:])
+
+        tiles_at_once = BANKS // 2
+        for first_tile in range(0, N_TILES, tiles_at_once):
+            group = range(first_tile, min(first_tile + tiles_at_once, N_TILES))
+            accs = {n: (bank(2 * (n % tiles_at_once), [P, S2]), bank(2 * (n % tiles_at_once) + 1, [P, S2])) for n in group}
+            for n in group:
+                message_pass(n, 0, accs[n][0])
+                gate_pass(n, 0, accs[n][1])
+            for n in group:
+                gate_pass(n, 1, accs[n][1])
+                message_pass(n, 1, accs[n][0])
+                finish(n, accs[n][0], accs[n][1])

@@ -32,6 +32,7 @@ N_TILES = N // P
 BANKS = 8
 LIST_COLS = PASS // 16
 RUN = 4
+WG_ORDER = ((0, 0), (0, 1), (1, 0), (1, 1), (0, 2), (1, 2))
 
 
 def tile_list_gated_graph_messages_kernel(
@@ -55,14 +56,15 @@ def tile_list_gated_graph_messages_kernel(
         nc.vector.memset(centre_scales[:].bitcast(I32), 0)
         nc.vector.memset(neigh_scales[:].bitcast(I32), 0)
         nc.vector.memset(msg_scales[:].bitcast(I32), 0)
-        for queue, tile, source in ((nc.scalar, centre_scales, tab2_scales), (nc.gpsimd, neigh_scales, tab_scales)):
+        for tile, source in ((centre_scales, tab2_scales), (neigh_scales, tab_scales)):
             for q in range(QUADRANTS):
-                queue.dma_start(
+                nc.scalar.dma_start(
                     out=tile[32 * q : 32 * q + SCALE_ROWS * K_PASSES, :].bitcast(I32),
                     in_=source[:, SCALE_ROWS * q : SCALE_ROWS * (q + 1), :].bitcast(I32),
                 )
-        for q in range(QUADRANTS):
-            nc.gpsimd.dma_start(
+
+        def load_msg_scales(q):
+            nc.sync.dma_start(
                 out=msg_scales[32 * q : 32 * q + SCALE_ROWS, :, :].bitcast(I32),
                 in_=m4_scales[:, SCALE_ROWS * q : SCALE_ROWS * (q + 1), :].rearrange("a r n -> r a n").bitcast(I32),
             )
@@ -91,17 +93,26 @@ def tile_list_gated_graph_messages_kernel(
         neigh_table = [load_words("neigh_table", tab_words, 0)]
         deg_cols = sbuf("deg_cols", [P, I_PASSES, PACK], F32)
         nc.sync.dma_start(out=deg_cols[:], in_=deg.rearrange("(b p t) -> p b t", p=P, t=PACK))
+        wg_rows = {(0, 0): load_wg(0, 0)}
+        load_msg_scales(0)
+        neigh_table.append(load_words("neigh_table", tab_words, 1))
+        load_msg_scales(1)
         adj_rows = [load_adj(0)]
-        neigh_table.extend(load_words("neigh_table", tab_words, a) for a in range(1, K_PASSES))
+        load_msg_scales(2)
+        neigh_table.append(load_words("neigh_table", tab_words, 2))
+        load_msg_scales(3)
         adj_rows.append(load_adj(1))
-        wg_rows = {(0, c): load_wg(0, c) for c in range(W_CHUNKS)}
+        wg_rows[(0, 1)] = load_wg(0, 1)
         msg_words = sbuf("msg_words", [P, I_PASSES, 2 * N], U8)
         nc.sync.dma_start(out=msg_words[:].bitcast(I32), in_=m4_words.rearrange("a p c -> p a c").bitcast(I32))
         bias_cols = sbuf("bias_cols", [P, N_TILES], F32)
         with nc.allow_non_contiguous_dma(reason="one bias value a partition"):
             nc.sync.dma_start(out=bias_cols[:], in_=bg.rearrange("(n p) -> p n", p=P))
-        for c in range(W_CHUNKS):
-            wg_rows[(1, c)] = load_wg(1, c)
+        for b, c in WG_ORDER[2:]:
+            wg_rows[(b, c)] = load_wg(b, c)
+
+        warm = sbuf("warm", [P, 1], F32)
+        nc.scalar.activation(warm[:], deg_cols[:, 0, 0:1], SIGMOID)
 
         centre_words = []
         for a in range(K_PASSES):
@@ -151,61 +162,70 @@ def tile_list_gated_graph_messages_kernel(
                             stop=(a == K_PASSES - 1 and t == PACK - 1),
                         )
 
-        h_codes, h_scales = [], []
-        for b in range(I_PASSES):
+        def interleaved(tile):
+            return tile.rearrange("p (r i) t -> p r t i", i=RUN)
+
+        def by_rows(tile):
+            return tile.rearrange("p t (r i) -> p r t i", i=RUN)
+
+        wg_codes, wg_scales = {}, {}
+
+        def quantise_wg(b, c):
+            wg_bf16 = sbuf("wg_bf16_%d_%d" % (b, c), [P, W_CHUNK, PACK], BF16)
+            if (b, c) == WG_ORDER[-1]:
+                nc.vector.tensor_copy(interleaved(wg_bf16[:]), by_rows(wg_rows[(b, c)][:]))
+            else:
+                nc.scalar.copy(interleaved(wg_bf16[:]), by_rows(wg_rows[(b, c)][:]))
+            codes = sbuf("wg_codes%d_%d" % (b, c), [P, W_CHUNK], U32)
+            scales = sbuf("wg_scales%d_%d" % (b, c), [P, W_CHUNK], U8)
+            nc.vector.quantize_mx(out=codes[:].bitcast(FP8X4), scales=scales[:], in_=wg_bf16[:].rearrange("p n t -> p (n t)"))
+            wg_codes[(b, c)] = codes
+            wg_scales[(b, c)] = scales
+
+        def make_h(b, pieces):
             weight = sbuf("edge_weight%d" % b, [P, PACK, S2], F32)
             for t in range(PACK):
                 nc.scalar.activation(weight[:, t, :], adj_rows[b][:, t, :], COPY, scale=deg_cols[:, b, t : t + 1])
             h_bf16 = sbuf("h_bf16_%d" % b, [P, S2, PACK], BF16)
             for c in range(J_CHUNKS):
                 cols = slice(c * J_CHUNK, (c + 1) * J_CHUNK)
-                nc.vector.tensor_tensor(
-                    h_bf16[:, cols, :].rearrange("p (r i) t -> p r t i", i=RUN),
-                    compare[(b, c)][:].rearrange("p t (r i) -> p r t i", i=RUN),
-                    weight[:, :, cols].rearrange("p t (r i) -> p r t i", i=RUN),
-                    MULT,
-                )
+                nc.vector.tensor_tensor(interleaved(h_bf16[:, cols, :]), by_rows(compare[(b, c)][:]), by_rows(weight[:, :, cols]), MULT)
             codes = sbuf("h_codes%d" % b, [P, S2], U32)
             scales = sbuf("h_scales%d" % b, [P, S2], U8)
-            nc.vector.quantize_mx(out=codes[:].bitcast(FP8X4), scales=scales[:], in_=h_bf16[:].rearrange("p j t -> p (j t)"))
-            h_codes.append(codes)
-            h_scales.append(scales)
-
-        wg_codes, wg_scales = {}, {}
-        for b in range(I_PASSES):
-            for c in range(W_CHUNKS):
-                wg_bf16 = sbuf("wg_bf16_%d_%d" % (b, c), [P, W_CHUNK, PACK], BF16)
-                nc.scalar.copy(
-                    wg_bf16[:].rearrange("p (r i) t -> p r t i", i=RUN),
-                    wg_rows[(b, c)][:].rearrange("p t (r i) -> p r t i", i=RUN),
+            for cols in pieces:
+                nc.vector.quantize_mx(
+                    out=codes[:, cols].bitcast(FP8X4), scales=scales[:, cols], in_=h_bf16[:, cols, :].rearrange("p j t -> p (j t)")
                 )
-                codes = sbuf("wg_codes%d_%d" % (b, c), [P, W_CHUNK], U32)
-                scales = sbuf("wg_scales%d_%d" % (b, c), [P, W_CHUNK], U8)
-                nc.vector.quantize_mx(out=codes[:].bitcast(FP8X4), scales=scales[:], in_=wg_bf16[:].rearrange("p n t -> p (n t)"))
-                wg_codes[(b, c)] = codes
-                wg_scales[(b, c)] = scales
+            return codes, scales
 
-        def message_pass(n, b, acc):
+        whole = [slice(0, S2)]
+        chunks = [slice(c * J_CHUNK, (c + 1) * J_CHUNK) for c in range(J_CHUNKS)]
+        quantise_wg(*WG_ORDER[0])
+        h_mx = [make_h(0, whole), make_h(1, chunks)]
+        for b, c in WG_ORDER[1:]:
+            quantise_wg(b, c)
+
+        def message_pass(n, b, acc, cols):
             nc.tensor.matmul_mx(
-                out=acc[:],
+                out=acc[:, cols],
                 lhsT=msg_words[:, b, 2 * P * n : 2 * P * (n + 1)].bitcast(FP4X4),
                 lhsT_scale=msg_scales[:, b, P * n : P * (n + 1)],
-                rhs=h_codes[b][:].bitcast(FP8X4),
-                rhs_scale=h_scales[b][:],
+                rhs=h_mx[b][0][:, cols].bitcast(FP8X4),
+                rhs_scale=h_mx[b][1][:, cols],
                 start=(b == 0),
-                stop=(b == I_PASSES - 1),
+                stop=(b == I_PASSES - 1 and cols.stop == S2),
             )
 
-        def gate_pass(n, b, acc):
+        def gate_pass(n, b, acc, cols):
             c, first = divmod(n * P, W_CHUNK)
             nc.tensor.matmul_mx(
-                out=acc[:],
+                out=acc[:, cols],
                 lhsT=wg_codes[(b, c)][:, first : first + P].bitcast(FP8X4),
                 lhsT_scale=wg_scales[(b, c)][:, first : first + P],
-                rhs=h_codes[b][:].bitcast(FP8X4),
-                rhs_scale=h_scales[b][:],
+                rhs=h_mx[b][0][:, cols].bitcast(FP8X4),
+                rhs_scale=h_mx[b][1][:, cols],
                 start=(b == 0),
-                stop=(b == I_PASSES - 1),
+                stop=(b == I_PASSES - 1 and cols.stop == S2),
             )
 
         def finish(n, y_acc, g_acc):
@@ -216,13 +236,15 @@ def tile_list_gated_graph_messages_kernel(
             nc.sync.dma_start(out=out[n * P : (n + 1) * P, :], in_=result[:])
 
         tiles_at_once = BANKS // 2
-        for first_tile in range(0, N_TILES, tiles_at_once):
+        for first_tile, pieces in ((0, chunks), (tiles_at_once, whole)):
             group = range(first_tile, min(first_tile + tiles_at_once, N_TILES))
-            accs = {n: (bank(2 * (n % tiles_at_once), [P, S2]), bank(2 * (n % tiles_at_once) + 1, [P, S2])) for n in group}
+            accs = {n: (bank(2 * (n % tiles_at_once) + 1, [P, S2]), bank(2 * (n % tiles_at_once), [P, S2])) for n in group}
             for n in group:
-                message_pass(n, 0, accs[n][0])
-                gate_pass(n, 0, accs[n][1])
+                gate_pass(n, 0, accs[n][1], whole[0])
+                message_pass(n, 0, accs[n][0], whole[0])
+            for cols in pieces:
+                for n in group:
+                    gate_pass(n, 1, accs[n][1], cols)
+                    message_pass(n, 1, accs[n][0], cols)
             for n in group:
-                gate_pass(n, 1, accs[n][1])
-                message_pass(n, 1, accs[n][0])
                 finish(n, accs[n][0], accs[n][1])

@@ -1,6 +1,7 @@
 from contextlib import ExitStack
 
 import concourse.mybir as mybir
+from concourse.masks import make_identity
 
 K, T, S, T2, S2, N = 1536, 2048, 1024, 1024, 512, 768
 FLOPS = 2 * K * S * S2 + 2 * 2 * S * N * S2
@@ -31,7 +32,6 @@ W_CHUNKS = N // W_CHUNK
 N_TILES = N // P
 BANKS = 8
 LIST_COLS = PASS // 16
-RUN = 4
 WG_ORDER = ((0, 0), (0, 1), (1, 0), (1, 1), (0, 2), (1, 2))
 
 
@@ -41,21 +41,19 @@ def tile_list_gated_graph_messages_kernel(
     nc = tc.nc
     with ExitStack() as ctx:
         lists = ctx.enter_context(tc.tile_pool(name="lists", bufs=1))
-        keep = ctx.enter_context(tc.tile_pool(name="keep", bufs=1))
+        early = ctx.enter_context(tc.tile_pool(name="early", bufs=1))
         psum = ctx.enter_context(tc.psum_pool(name="psum", bufs=1))
 
-        def sbuf(name, shape, dtype):
-            return keep.tile(shape, dtype, name=name, align_bytes=64)
+        def tile_in(pool, name, shape, dtype, tag=None):
+            return pool.tile(shape, dtype, name=name, tag=tag or name, align_bytes=64)
 
         def bank(index, shape):
             return psum.tile(shape, F32, name="bank", tag="bank%d" % index)
 
-        centre_scales = sbuf("centre_scales", [P, T2], U8)
-        neigh_scales = sbuf("neigh_scales", [P, T], U8)
-        msg_scales = sbuf("msg_scales", [P, I_PASSES, N], U8)
+        centre_scales = tile_in(early, "centre_scales", [P, T2], U8)
+        neigh_scales = tile_in(early, "neigh_scales", [P, T], U8)
         nc.vector.memset(centre_scales[:].bitcast(I32), 0)
         nc.vector.memset(neigh_scales[:].bitcast(I32), 0)
-        nc.vector.memset(msg_scales[:].bitcast(I32), 0)
         for tile, source in ((centre_scales, tab2_scales), (neigh_scales, tab_scales)):
             for q in range(QUADRANTS):
                 nc.scalar.dma_start(
@@ -69,8 +67,8 @@ def tile_list_gated_graph_messages_kernel(
                 in_=m4_scales[:, SCALE_ROWS * q : SCALE_ROWS * (q + 1), :].rearrange("a r n -> r a n").bitcast(I32),
             )
 
-        def load_words(name, source, a):
-            words = sbuf("%s%d" % (name, a), [P, source.shape[2]], U32)
+        def load_words(pool, name, source, a):
+            words = tile_in(pool, "%s%d" % (name, a), [P, source.shape[2]], U32)
             nc.sync.dma_start(out=words[:].bitcast(I32), in_=source[a].rearrange("p n t -> p (n t)").bitcast(I32))
             return words
 
@@ -79,46 +77,68 @@ def tile_list_gated_graph_messages_kernel(
             nc.sync.dma_start(out=rows[:], in_=adj[b * PASS : (b + 1) * PASS, :].rearrange("(p t) j -> p t j", t=PACK))
             return rows
 
-        def load_wg(b, c):
-            rows = sbuf("wg%d_%d" % (b, c), [P, PACK, W_CHUNK], F32)
-            source = wg[b * PASS : (b + 1) * PASS, c * W_CHUNK : (c + 1) * W_CHUNK]
+        wg_rows = {}
+
+        def load_wg(b, first, count):
+            rows = sbuf("wg%d_%d" % (b, first), [P, PACK, count * W_CHUNK], F32)
+            source = wg[b * PASS : (b + 1) * PASS, first * W_CHUNK : (first + count) * W_CHUNK]
             nc.sync.dma_start(out=rows[:], in_=source.rearrange("(p t) n -> p t n", t=PACK))
-            return rows
+            for c in range(count):
+                wg_rows[(b, first + c)] = rows[:, :, c * W_CHUNK : (c + 1) * W_CHUNK]
 
         centre_list = lists.tile([P, S2 // 16], U16, name="centre_list")
         neigh_list = lists.tile([P, S // 16], U16, name="neigh_list")
         nc.sync.dma_start(centre_list[:], offs2)
-        centre_table = [load_words("centre_table", tab2_words, a) for a in range(K_PASSES)]
-        nc.sync.dma_start(neigh_list[:], offs)
-        neigh_table = [load_words("neigh_table", tab_words, 0)]
+        identity = tile_in(early, "identity", [P, P], F32)
+        bias_rows = tile_in(early, "bias_rows", [P, P], F32)
+        nc.gpsimd.memset(bias_rows[:], 0.0)
+        make_identity(nc, identity[:])
+
+        def gather_centre_words(a, table):
+            picked = tile_in(early, "centre_words%d" % a, [P, S2], U32)
+            nc.vector.tensor_copy(picked[:], table[:].indirect(centre_list[:]))
+            return picked
+
+        with tc.tile_pool(name="first", bufs=1) as first:
+            first_table = load_words(first, "centre_table", tab2_words, 0)
+            nc.sync.dma_start(neigh_list[:], offs)
+            later_tables = [load_words(early, "centre_table", tab2_words, a) for a in range(1, K_PASSES)]
+            nc.sync.dma_start(out=bias_rows[0:N_TILES, :], in_=bg.rearrange("(n p) -> n p", p=P))
+            centre_words = [gather_centre_words(0, first_table)]
+
+        rest = ctx.enter_context(tc.tile_pool(name="rest", bufs=1))
+
+        def sbuf(name, shape, dtype, tag=None):
+            return tile_in(rest, name, shape, dtype, tag)
+
+        msg_scales = sbuf("msg_scales", [P, I_PASSES, N], U8)
+        nc.vector.memset(msg_scales[:].bitcast(I32), 0)
+        neigh_table = [load_words(rest, "neigh_table", tab_words, 0)]
         deg_cols = sbuf("deg_cols", [P, I_PASSES, PACK], F32)
         nc.sync.dma_start(out=deg_cols[:], in_=deg.rearrange("(b p t) -> p b t", p=P, t=PACK))
-        wg_rows = {(0, 0): load_wg(0, 0)}
-        load_msg_scales(0)
-        neigh_table.append(load_words("neigh_table", tab_words, 1))
-        load_msg_scales(1)
+        load_wg(0, 0, 1)
+        neigh_table.append(load_words(rest, "neigh_table", tab_words, 1))
         adj_rows = [load_adj(0)]
-        load_msg_scales(2)
-        neigh_table.append(load_words("neigh_table", tab_words, 2))
-        load_msg_scales(3)
+        neigh_table.append(load_words(rest, "neigh_table", tab_words, 2))
+        for q in range(QUADRANTS):
+            load_msg_scales(q)
         adj_rows.append(load_adj(1))
-        wg_rows[(0, 1)] = load_wg(0, 1)
+        load_wg(0, 1, 1)
         msg_words = sbuf("msg_words", [P, I_PASSES, 2 * N], U8)
         nc.sync.dma_start(out=msg_words[:].bitcast(I32), in_=m4_words.rearrange("a p c -> p a c").bitcast(I32))
+        load_wg(1, 0, 2)
+        load_wg(0, 2, 1)
+        load_wg(1, 2, 1)
+
+        bias_turned = bank(BANKS - 1, [P, P])
+        nc.tensor.transpose(bias_turned[:], bias_rows[:], identity[:])
         bias_cols = sbuf("bias_cols", [P, N_TILES], F32)
-        with nc.allow_non_contiguous_dma(reason="one bias value a partition"):
-            nc.sync.dma_start(out=bias_cols[:], in_=bg.rearrange("(n p) -> p n", p=P))
-        for b, c in WG_ORDER[2:]:
-            wg_rows[(b, c)] = load_wg(b, c)
+        nc.scalar.copy(bias_cols[:], bias_turned[:, 0:N_TILES])
 
         warm = sbuf("warm", [P, 1], F32)
         nc.scalar.activation(warm[:], deg_cols[:, 0, 0:1], SIGMOID)
 
-        centre_words = []
-        for a in range(K_PASSES):
-            picked = sbuf("centre_words%d" % a, [P, S2], U32)
-            nc.vector.tensor_copy(picked[:], centre_table[a][:].indirect(centre_list[:]))
-            centre_words.append(picked)
+        centre_words.extend(gather_centre_words(a, later_tables[a - 1]) for a in range(1, K_PASSES))
         centre_bytes = sbuf("centre_bytes", [P, S2], U8)
         nc.vector.tensor_copy(centre_bytes[:], centre_scales[:].indirect(centre_list[:]))
 
@@ -130,19 +150,15 @@ def tile_list_gated_graph_messages_kernel(
             nc.vector.tensor_copy(picked[:].rearrange("p t m -> p m t"), neigh_table[a][:].indirect(part_of_list(b)))
             return picked
 
-        def gather_neigh_bytes(b):
-            picked = sbuf("neigh_picked%d" % b, [P, PASS], U8)
-            nc.vector.tensor_copy(picked[:], neigh_scales[:].indirect(part_of_list(b)))
-            return picked
-
-        def deal_neigh_bytes(b, picked):
-            dealt = sbuf("neigh_bytes%d" % b, [P, PACK, P], U8)
-            nc.vector.tensor_copy(dealt[:], picked[:].rearrange("p (m t) -> p t m", t=PACK))
-            return dealt
-
         neigh_words = {(0, b): gather_neigh_words(0, b) for b in range(I_PASSES)}
-        picked_bytes = [gather_neigh_bytes(b) for b in range(I_PASSES)]
-        neigh_bytes = [deal_neigh_bytes(b, picked_bytes[b]) for b in range(I_PASSES)]
+        picked_bytes = sbuf("picked_bytes", [P, I_PASSES, PASS], U8, tag="neigh_table0")
+        neigh_bytes = []
+        for b in range(I_PASSES):
+            nc.vector.tensor_copy(picked_bytes[:, b, :], neigh_scales[:].indirect(part_of_list(b)))
+        for b in range(I_PASSES):
+            dealt = sbuf("neigh_bytes%d" % b, [P, PACK, P], U8)
+            nc.vector.tensor_copy(dealt[:], picked_bytes[:, b, :].rearrange("p (m t) -> p t m", t=PACK))
+            neigh_bytes.append(dealt)
 
         compare = {(b, c): bank(b * J_CHUNKS + c, [P, PACK, J_CHUNK]) for b in range(I_PASSES) for c in range(J_CHUNKS)}
         for a in range(K_PASSES):
@@ -162,47 +178,62 @@ def tile_list_gated_graph_messages_kernel(
                             stop=(a == K_PASSES - 1 and t == PACK - 1),
                         )
 
-        def interleaved(tile):
-            return tile.rearrange("p (r i) t -> p r t i", i=RUN)
+        def interleaved(tile, run):
+            return tile.rearrange("p (r i) t -> p r t i", i=run)
 
-        def by_rows(tile):
-            return tile.rearrange("p t (r i) -> p r t i", i=RUN)
+        def by_rows(tile, run):
+            return tile.rearrange("p t (r i) -> p r t i", i=run)
 
         wg_codes, wg_scales = {}, {}
 
         def quantise_wg(b, c):
             wg_bf16 = sbuf("wg_bf16_%d_%d" % (b, c), [P, W_CHUNK, PACK], BF16)
             if (b, c) == WG_ORDER[-1]:
-                nc.vector.tensor_copy(interleaved(wg_bf16[:]), by_rows(wg_rows[(b, c)][:]))
+                nc.vector.tensor_copy(interleaved(wg_bf16[:], 4), by_rows(wg_rows[(b, c)], 4))
             else:
-                nc.scalar.copy(interleaved(wg_bf16[:]), by_rows(wg_rows[(b, c)][:]))
+                nc.scalar.copy(interleaved(wg_bf16[:], 4), by_rows(wg_rows[(b, c)], 4))
             codes = sbuf("wg_codes%d_%d" % (b, c), [P, W_CHUNK], U32)
             scales = sbuf("wg_scales%d_%d" % (b, c), [P, W_CHUNK], U8)
             nc.vector.quantize_mx(out=codes[:].bitcast(FP8X4), scales=scales[:], in_=wg_bf16[:].rearrange("p n t -> p (n t)"))
             wg_codes[(b, c)] = codes
             wg_scales[(b, c)] = scales
 
-        def make_h(b, pieces):
+        def weigh_edges(b):
             weight = sbuf("edge_weight%d" % b, [P, PACK, S2], F32)
             for t in range(PACK):
                 nc.scalar.activation(weight[:, t, :], adj_rows[b][:, t, :], COPY, scale=deg_cols[:, b, t : t + 1])
+            return weight
+
+        def make_h(b, weight, pieces):
             h_bf16 = sbuf("h_bf16_%d" % b, [P, S2, PACK], BF16)
-            for c in range(J_CHUNKS):
-                cols = slice(c * J_CHUNK, (c + 1) * J_CHUNK)
-                nc.vector.tensor_tensor(interleaved(h_bf16[:, cols, :]), by_rows(compare[(b, c)][:]), by_rows(weight[:, :, cols]), MULT)
             codes = sbuf("h_codes%d" % b, [P, S2], U32)
             scales = sbuf("h_scales%d" % b, [P, S2], U8)
-            for cols in pieces:
+
+            def quantise(cols):
                 nc.vector.quantize_mx(
                     out=codes[:, cols].bitcast(FP8X4), scales=scales[:, cols], in_=h_bf16[:, cols, :].rearrange("p j t -> p (j t)")
                 )
+
+            done = 0
+            for c, cols in enumerate(chunks):
+                nc.vector.tensor_tensor(
+                    interleaved(h_bf16[:, cols, :], 2), by_rows(compare[(b, c)][:], 2), by_rows(weight[:, :, cols], 2), MULT
+                )
+                if pieces[done].stop <= cols.start:
+                    quantise(pieces[done])
+                    done = done + 1
+            for cols in pieces[done:]:
+                quantise(cols)
             return codes, scales
 
         whole = [slice(0, S2)]
         chunks = [slice(c * J_CHUNK, (c + 1) * J_CHUNK) for c in range(J_CHUNKS)]
         quantise_wg(*WG_ORDER[0])
-        h_mx = [make_h(0, whole), make_h(1, chunks)]
-        for b, c in WG_ORDER[1:]:
+        weights = [weigh_edges(b) for b in range(I_PASSES)]
+        h_mx = [make_h(0, weights[0], whole)]
+        quantise_wg(*WG_ORDER[1])
+        h_mx.append(make_h(1, weights[1], chunks))
+        for b, c in WG_ORDER[2:]:
             quantise_wg(b, c)
 
         def message_pass(n, b, acc, cols):
@@ -244,7 +275,7 @@ def tile_list_gated_graph_messages_kernel(
                 message_pass(n, 0, accs[n][0], whole[0])
             for cols in pieces:
                 for n in group:
-                    gate_pass(n, 1, accs[n][1], cols)
                     message_pass(n, 1, accs[n][0], cols)
             for n in group:
+                gate_pass(n, 1, accs[n][1], whole[0])
                 finish(n, accs[n][0], accs[n][1])

@@ -1,7 +1,6 @@
 from contextlib import ExitStack
 
 import concourse.mybir as mybir
-from concourse.masks import make_identity
 
 K, T, S, T2, S2, N = 1536, 2048, 1024, 1024, 512, 768
 FLOPS = 2 * K * S * S2 + 2 * 2 * S * N * S2
@@ -15,6 +14,7 @@ U8 = mybir.dt.uint8
 FP8X4 = mybir.dt.float8_e4m3fn_x4
 FP4X4 = mybir.dt.float4_e2m1fn_x4
 MULT = mybir.AluOpType.mult
+NOT_EQUAL = mybir.AluOpType.not_equal
 COPY = mybir.ActivationFunctionType.Copy
 SIGMOID = mybir.ActivationFunctionType.Sigmoid
 
@@ -32,7 +32,7 @@ W_CHUNKS = N // W_CHUNK
 N_TILES = N // P
 BANKS = 8
 LIST_COLS = PASS // 16
-WG_ORDER = ((0, 0), (0, 1), (1, 0), (1, 1), (0, 2), (1, 2))
+WG_ORDER = ((0, 0), (1, 0), (1, 1), (0, 1), (0, 2), (1, 2))
 
 
 def tile_list_gated_graph_messages_kernel(
@@ -52,20 +52,23 @@ def tile_list_gated_graph_messages_kernel(
 
         centre_scales = tile_in(early, "centre_scales", [P, T2], U8)
         neigh_scales = tile_in(early, "neigh_scales", [P, T], U8)
-        nc.vector.memset(centre_scales[:].bitcast(I32), 0)
-        nc.vector.memset(neigh_scales[:].bitcast(I32), 0)
-        for tile, source in ((centre_scales, tab2_scales), (neigh_scales, tab_scales)):
+        msg_scales = tile_in(early, "msg_scales", [P, I_PASSES, N], U8)
+        identity = tile_in(early, "identity", [P, P], F32)
+        bias_rows = tile_in(early, "bias_rows", [P, P], F32)
+
+        def load_table_scales(queue, tile, source):
             for q in range(QUADRANTS):
-                nc.scalar.dma_start(
+                queue.dma_start(
                     out=tile[32 * q : 32 * q + SCALE_ROWS * K_PASSES, :].bitcast(I32),
                     in_=source[:, SCALE_ROWS * q : SCALE_ROWS * (q + 1), :].bitcast(I32),
                 )
 
-        def load_msg_scales(q):
-            nc.sync.dma_start(
-                out=msg_scales[32 * q : 32 * q + SCALE_ROWS, :, :].bitcast(I32),
-                in_=m4_scales[:, SCALE_ROWS * q : SCALE_ROWS * (q + 1), :].rearrange("a r n -> r a n").bitcast(I32),
-            )
+        def load_msg_scales(queue):
+            for q in range(QUADRANTS):
+                queue.dma_start(
+                    out=msg_scales[32 * q : 32 * q + SCALE_ROWS, :, :].bitcast(I32),
+                    in_=m4_scales[:, SCALE_ROWS * q : SCALE_ROWS * (q + 1), :].rearrange("a r n -> r a n").bitcast(I32),
+                )
 
         def load_words(pool, name, source, a):
             words = tile_in(pool, "%s%d" % (name, a), [P, source.shape[2]], U32)
@@ -89,45 +92,41 @@ def tile_list_gated_graph_messages_kernel(
         centre_list = lists.tile([P, S2 // 16], U16, name="centre_list")
         neigh_list = lists.tile([P, S // 16], U16, name="neigh_list")
         nc.sync.dma_start(centre_list[:], offs2)
-        identity = tile_in(early, "identity", [P, P], F32)
-        bias_rows = tile_in(early, "bias_rows", [P, P], F32)
-        nc.gpsimd.memset(bias_rows[:], 0.0)
-        make_identity(nc, identity[:])
+        centre_table = [load_words(early, "centre_table", tab2_words, a) for a in range(K_PASSES - 1)]
+        nc.sync.dma_start(neigh_list[:], offs)
 
-        def gather_centre_words(a, table):
-            picked = tile_in(early, "centre_words%d" % a, [P, S2], U32)
-            nc.vector.tensor_copy(picked[:], table[:].indirect(centre_list[:]))
-            return picked
-
+        nc.vector.memset(centre_scales[:].bitcast(I32), 0)
+        load_table_scales(nc.scalar, centre_scales, tab2_scales)
+        nc.vector.memset(neigh_scales[:].bitcast(I32), 0)
+        load_table_scales(nc.scalar, neigh_scales, tab_scales)
         with tc.tile_pool(name="first", bufs=1) as first:
-            first_table = load_words(first, "centre_table", tab2_words, 0)
-            nc.sync.dma_start(neigh_list[:], offs)
-            later_tables = [load_words(early, "centre_table", tab2_words, a) for a in range(1, K_PASSES)]
-            nc.sync.dma_start(out=bias_rows[0:N_TILES, :], in_=bg.rearrange("(n p) -> n p", p=P))
-            centre_words = [gather_centre_words(0, first_table)]
+            zeros = tile_in(first, "zeros", [P, P], F32)
+            nc.vector.memset(zeros[:], 0.0)
+            nc.gpsimd.affine_select(
+                out=identity[:], in_=zeros[:], compare_op=NOT_EQUAL, fill=1.0, base=0, pattern=[[-1, P]], channel_multiplier=1
+            )
+        nc.vector.memset(msg_scales[:].bitcast(I32), 0)
+        load_msg_scales(nc.scalar)
+        nc.vector.memset(bias_rows[:], 0.0)
 
         rest = ctx.enter_context(tc.tile_pool(name="rest", bufs=1))
 
         def sbuf(name, shape, dtype, tag=None):
             return tile_in(rest, name, shape, dtype, tag)
 
-        msg_scales = sbuf("msg_scales", [P, I_PASSES, N], U8)
-        nc.vector.memset(msg_scales[:].bitcast(I32), 0)
+        centre_table.append(load_words(rest, "centre_table", tab2_words, K_PASSES - 1))
         neigh_table = [load_words(rest, "neigh_table", tab_words, 0)]
         deg_cols = sbuf("deg_cols", [P, I_PASSES, PACK], F32)
         nc.sync.dma_start(out=deg_cols[:], in_=deg.rearrange("(b p t) -> p b t", p=P, t=PACK))
         load_wg(0, 0, 1)
-        neigh_table.append(load_words(rest, "neigh_table", tab_words, 1))
         adj_rows = [load_adj(0)]
-        neigh_table.append(load_words(rest, "neigh_table", tab_words, 2))
-        for q in range(QUADRANTS):
-            load_msg_scales(q)
+        neigh_table.extend(load_words(rest, "neigh_table", tab_words, a) for a in range(1, K_PASSES))
         adj_rows.append(load_adj(1))
-        load_wg(0, 1, 1)
+        nc.sync.dma_start(out=bias_rows[0:N_TILES, :], in_=bg.rearrange("(n p) -> n p", p=P))
         msg_words = sbuf("msg_words", [P, I_PASSES, 2 * N], U8)
         nc.sync.dma_start(out=msg_words[:].bitcast(I32), in_=m4_words.rearrange("a p c -> p a c").bitcast(I32))
         load_wg(1, 0, 2)
-        load_wg(0, 2, 1)
+        load_wg(0, 1, 2)
         load_wg(1, 2, 1)
 
         bias_turned = bank(BANKS - 1, [P, P])
@@ -138,33 +137,38 @@ def tile_list_gated_graph_messages_kernel(
         warm = sbuf("warm", [P, 1], F32)
         nc.scalar.activation(warm[:], deg_cols[:, 0, 0:1], SIGMOID)
 
-        centre_words.extend(gather_centre_words(a, later_tables[a - 1]) for a in range(1, K_PASSES))
+        centre_words = []
+        for a in range(K_PASSES):
+            picked = sbuf("centre_words%d" % a, [P, S2], U32) if a == K_PASSES - 1 else tile_in(early, "centre_words%d" % a, [P, S2], U32)
+            nc.vector.tensor_copy(picked[:], centre_table[a][:].indirect(centre_list[:]))
+            centre_words.append(picked)
         centre_bytes = sbuf("centre_bytes", [P, S2], U8)
         nc.vector.tensor_copy(centre_bytes[:], centre_scales[:].indirect(centre_list[:]))
 
         def part_of_list(b):
             return neigh_list[:, b * LIST_COLS : (b + 1) * LIST_COLS]
 
-        def gather_neigh_words(a, b):
-            picked = sbuf("neigh_words%d_%d" % (a, b), [P, PACK, P], U32)
-            nc.vector.tensor_copy(picked[:].rearrange("p t m -> p m t"), neigh_table[a][:].indirect(part_of_list(b)))
+        def gather_neigh_words(a, b, picked):
+            nc.vector.tensor_copy(picked.rearrange("p t m -> p m t"), neigh_table[a][:].indirect(part_of_list(b)))
             return picked
 
-        neigh_words = {(0, b): gather_neigh_words(0, b) for b in range(I_PASSES)}
-        picked_bytes = sbuf("picked_bytes", [P, I_PASSES, PASS], U8, tag="neigh_table0")
-        neigh_bytes = []
+        neigh_words = {}
+        picked_bytes = [sbuf("picked_bytes%d" % b, [P, PASS], U8) for b in range(I_PASSES)]
+        neigh_bytes = [sbuf("neigh_bytes%d" % b, [P, PACK, P], U8) for b in range(I_PASSES)]
         for b in range(I_PASSES):
-            nc.vector.tensor_copy(picked_bytes[:, b, :], neigh_scales[:].indirect(part_of_list(b)))
+            nc.vector.tensor_copy(picked_bytes[b][:], neigh_scales[:].indirect(part_of_list(b)))
         for b in range(I_PASSES):
-            dealt = sbuf("neigh_bytes%d" % b, [P, PACK, P], U8)
-            nc.vector.tensor_copy(dealt[:], picked_bytes[:, b, :].rearrange("p (m t) -> p t m", t=PACK))
-            neigh_bytes.append(dealt)
+            nc.vector.tensor_copy(neigh_bytes[b][:], picked_bytes[b][:].rearrange("p (m t) -> p t m", t=PACK))
+            neigh_words[(0, b)] = gather_neigh_words(0, b, sbuf("neigh_words0_%d" % b, [P, PACK, P], U32)[:])
+        for b in range(I_PASSES):
+            neigh_words[(1, b)] = gather_neigh_words(1, b, sbuf("neigh_words1_%d" % b, [P, PACK, P], U32, tag="picked_bytes%d" % b)[:])
+        last_words = tile_in(early, "neigh_words2", [P, I_PASSES, PACK, P], U32, tag="neigh_scales")
+        for b in range(I_PASSES):
+            neigh_words[(2, b)] = gather_neigh_words(2, b, last_words[:, b, :, :])
 
         compare = {(b, c): bank(b * J_CHUNKS + c, [P, PACK, J_CHUNK]) for b in range(I_PASSES) for c in range(J_CHUNKS)}
         for a in range(K_PASSES):
             for b in range(I_PASSES):
-                if a > 0:
-                    neigh_words[(a, b)] = gather_neigh_words(a, b)
                 for c in range(J_CHUNKS):
                     cols = slice(c * J_CHUNK, (c + 1) * J_CHUNK)
                     for t in range(PACK):
@@ -267,15 +271,24 @@ def tile_list_gated_graph_messages_kernel(
             nc.sync.dma_start(out=out[n * P : (n + 1) * P, :], in_=result[:])
 
         tiles_at_once = BANKS // 2
-        for first_tile, pieces in ((0, chunks), (tiles_at_once, whole)):
-            group = range(first_tile, min(first_tile + tiles_at_once, N_TILES))
-            accs = {n: (bank(2 * (n % tiles_at_once) + 1, [P, S2]), bank(2 * (n % tiles_at_once), [P, S2])) for n in group}
-            for n in group:
-                gate_pass(n, 0, accs[n][1], whole[0])
-                message_pass(n, 0, accs[n][0], whole[0])
-            for cols in pieces:
-                for n in group:
-                    message_pass(n, 1, accs[n][0], cols)
-            for n in group:
-                gate_pass(n, 1, accs[n][1], whole[0])
-                finish(n, accs[n][0], accs[n][1])
+
+        def accumulators(n):
+            return bank(2 * (n % tiles_at_once) + 1, [P, S2]), bank(2 * (n % tiles_at_once), [P, S2])
+
+        accs = [accumulators(n) for n in range(tiles_at_once)]
+        for n, (y_acc, g_acc) in enumerate(accs):
+            gate_pass(n, 0, g_acc, whole[0])
+            message_pass(n, 0, y_acc, whole[0])
+        for cols in chunks:
+            for n, (y_acc, g_acc) in enumerate(accs):
+                message_pass(n, 1, y_acc, cols)
+        for n, (y_acc, g_acc) in enumerate(accs):
+            gate_pass(n, 1, g_acc, whole[0])
+            finish(n, y_acc, g_acc)
+        for n in range(tiles_at_once, N_TILES):
+            y_acc, g_acc = accumulators(n)
+            for b in range(I_PASSES):
+                gate_pass(n, b, g_acc, whole[0])
+            for b in range(I_PASSES):
+                message_pass(n, b, y_acc, whole[0])
+            finish(n, y_acc, g_acc)

@@ -32,7 +32,7 @@ W_CHUNKS = N // W_CHUNK
 N_TILES = N // P
 BANKS = 8
 LIST_COLS = PASS // 16
-WG_ORDER = ((0, 0), (1, 0), (1, 1), (0, 1), (0, 2), (1, 2))
+WG_ORDER = ((0, 0), (0, 1), (1, 0), (1, 1), (0, 2), (1, 2))
 
 
 def tile_list_gated_graph_messages_kernel(
@@ -52,7 +52,6 @@ def tile_list_gated_graph_messages_kernel(
 
         centre_scales = tile_in(early, "centre_scales", [P, T2], U8)
         neigh_scales = tile_in(early, "neigh_scales", [P, T], U8)
-        msg_scales = tile_in(early, "msg_scales", [P, I_PASSES, N], U8)
         identity = tile_in(early, "identity", [P, P], F32)
         bias_rows = tile_in(early, "bias_rows", [P, P], F32)
 
@@ -75,15 +74,15 @@ def tile_list_gated_graph_messages_kernel(
             nc.sync.dma_start(out=words[:].bitcast(I32), in_=source[a].rearrange("p n t -> p (n t)").bitcast(I32))
             return words
 
-        def load_adj(b):
-            rows = sbuf("adj%d" % b, [P, PACK, S2], F32)
+        def load_adj(b, pool, tag=None):
+            rows = tile_in(pool, "adj%d" % b, [P, PACK, S2], F32, tag)
             nc.sync.dma_start(out=rows[:], in_=adj[b * PASS : (b + 1) * PASS, :].rearrange("(p t) j -> p t j", t=PACK))
             return rows
 
         wg_rows = {}
 
-        def load_wg(b, first, count):
-            rows = sbuf("wg%d_%d" % (b, first), [P, PACK, count * W_CHUNK], F32)
+        def load_wg(b, first, count, pool, tag=None):
+            rows = tile_in(pool, "wg%d_%d" % (b, first), [P, PACK, count * W_CHUNK], F32, tag)
             source = wg[b * PASS : (b + 1) * PASS, first * W_CHUNK : (first + count) * W_CHUNK]
             nc.sync.dma_start(out=rows[:], in_=source.rearrange("(p t) n -> p t n", t=PACK))
             for c in range(count):
@@ -92,42 +91,37 @@ def tile_list_gated_graph_messages_kernel(
         centre_list = lists.tile([P, S2 // 16], U16, name="centre_list")
         neigh_list = lists.tile([P, S // 16], U16, name="neigh_list")
         nc.sync.dma_start(centre_list[:], offs2)
-        centre_table = [load_words(early, "centre_table", tab2_words, a) for a in range(K_PASSES - 1)]
+        centre_table = [load_words(early, "centre_table", tab2_words, a) for a in range(K_PASSES)]
         nc.sync.dma_start(neigh_list[:], offs)
 
         nc.vector.memset(centre_scales[:].bitcast(I32), 0)
         load_table_scales(nc.scalar, centre_scales, tab2_scales)
-        nc.vector.memset(neigh_scales[:].bitcast(I32), 0)
-        load_table_scales(nc.scalar, neigh_scales, tab_scales)
         with tc.tile_pool(name="first", bufs=1) as first:
             zeros = tile_in(first, "zeros", [P, P], F32)
             nc.vector.memset(zeros[:], 0.0)
             nc.gpsimd.affine_select(
                 out=identity[:], in_=zeros[:], compare_op=NOT_EQUAL, fill=1.0, base=0, pattern=[[-1, P]], channel_multiplier=1
             )
-        nc.vector.memset(msg_scales[:].bitcast(I32), 0)
-        load_msg_scales(nc.scalar)
+        nc.vector.memset(neigh_scales[:].bitcast(I32), 0)
+        load_table_scales(nc.gpsimd, neigh_scales, tab_scales)
         nc.vector.memset(bias_rows[:], 0.0)
+        nc.scalar.dma_start(out=bias_rows[0:N_TILES, :], in_=bg.rearrange("(n p) -> n p", p=P))
 
         rest = ctx.enter_context(tc.tile_pool(name="rest", bufs=1))
 
         def sbuf(name, shape, dtype, tag=None):
             return tile_in(rest, name, shape, dtype, tag)
 
-        centre_table.append(load_words(rest, "centre_table", tab2_words, K_PASSES - 1))
+        msg_scales = sbuf("msg_scales", [P, I_PASSES, N], U8)
+        nc.vector.memset(msg_scales[:].bitcast(I32), 0)
         neigh_table = [load_words(rest, "neigh_table", tab_words, 0)]
         deg_cols = sbuf("deg_cols", [P, I_PASSES, PACK], F32)
         nc.sync.dma_start(out=deg_cols[:], in_=deg.rearrange("(b p t) -> p b t", p=P, t=PACK))
-        load_wg(0, 0, 1)
-        adj_rows = [load_adj(0)]
+        load_wg(0, 0, 1, rest)
+        adj_rows = [load_adj(0, rest)]
         neigh_table.extend(load_words(rest, "neigh_table", tab_words, a) for a in range(1, K_PASSES))
-        adj_rows.append(load_adj(1))
-        nc.sync.dma_start(out=bias_rows[0:N_TILES, :], in_=bg.rearrange("(n p) -> n p", p=P))
-        msg_words = sbuf("msg_words", [P, I_PASSES, 2 * N], U8)
-        nc.sync.dma_start(out=msg_words[:].bitcast(I32), in_=m4_words.rearrange("a p c -> p a c").bitcast(I32))
-        load_wg(1, 0, 2)
-        load_wg(0, 1, 2)
-        load_wg(1, 2, 1)
+        adj_rows.append(load_adj(1, rest))
+        load_msg_scales(nc.sync)
 
         bias_turned = bank(BANKS - 1, [P, P])
         nc.tensor.transpose(bias_turned[:], bias_rows[:], identity[:])
@@ -139,11 +133,17 @@ def tile_list_gated_graph_messages_kernel(
 
         centre_words = []
         for a in range(K_PASSES):
-            picked = sbuf("centre_words%d" % a, [P, S2], U32) if a == K_PASSES - 1 else tile_in(early, "centre_words%d" % a, [P, S2], U32)
+            picked = sbuf("centre_words%d" % a, [P, S2], U32)
             nc.vector.tensor_copy(picked[:], centre_table[a][:].indirect(centre_list[:]))
             centre_words.append(picked)
         centre_bytes = sbuf("centre_bytes", [P, S2], U8)
         nc.vector.tensor_copy(centre_bytes[:], centre_scales[:].indirect(centre_list[:]))
+
+        msg_words = tile_in(early, "msg_words", [P, I_PASSES, 2 * N], U8, "centre_table0")
+        nc.sync.dma_start(out=msg_words[:].bitcast(I32), in_=m4_words.rearrange("a p c -> p a c").bitcast(I32))
+        load_wg(0, 1, 1, early, "centre_table1")
+        load_wg(1, 0, 1, early, "centre_table2")
+        load_wg(1, 1, 1, early, "centre_scales")
 
         def part_of_list(b):
             return neigh_list[:, b * LIST_COLS : (b + 1) * LIST_COLS]
@@ -157,14 +157,15 @@ def tile_list_gated_graph_messages_kernel(
         neigh_bytes = [sbuf("neigh_bytes%d" % b, [P, PACK, P], U8) for b in range(I_PASSES)]
         for b in range(I_PASSES):
             nc.vector.tensor_copy(picked_bytes[b][:], neigh_scales[:].indirect(part_of_list(b)))
-        for b in range(I_PASSES):
+            first_words = sbuf("neigh_words0_%d" % b, [P, PACK, P], U32, tag=(None, "picked_bytes0")[b])
+            neigh_words[(0, b)] = gather_neigh_words(0, b, first_words[:])
             nc.vector.tensor_copy(neigh_bytes[b][:], picked_bytes[b][:].rearrange("p (m t) -> p t m", t=PACK))
-            neigh_words[(0, b)] = gather_neigh_words(0, b, sbuf("neigh_words0_%d" % b, [P, PACK, P], U32)[:])
-        for b in range(I_PASSES):
-            neigh_words[(1, b)] = gather_neigh_words(1, b, sbuf("neigh_words1_%d" % b, [P, PACK, P], U32, tag="picked_bytes%d" % b)[:])
-        last_words = tile_in(early, "neigh_words2", [P, I_PASSES, PACK, P], U32, tag="neigh_scales")
-        for b in range(I_PASSES):
-            neigh_words[(2, b)] = gather_neigh_words(2, b, last_words[:, b, :, :])
+        for a in range(1, K_PASSES):
+            for b in range(I_PASSES):
+                tag = ("picked_bytes1", "neigh_table0")[b] if a == 1 else None
+                later_words = sbuf("neigh_words%d_%d" % (a, b), [P, PACK, P], U32, tag=tag)
+                neigh_words[(a, b)] = gather_neigh_words(a, b, later_words[:])
+            load_wg(a - 1, W_CHUNKS - 1, 1, rest, "neigh_table%d" % a)
 
         compare = {(b, c): bank(b * J_CHUNKS + c, [P, PACK, J_CHUNK]) for b in range(I_PASSES) for c in range(J_CHUNKS)}
         for a in range(K_PASSES):
@@ -204,40 +205,40 @@ def tile_list_gated_graph_messages_kernel(
 
         def weigh_edges(b):
             weight = sbuf("edge_weight%d" % b, [P, PACK, S2], F32)
-            for t in range(PACK):
-                nc.scalar.activation(weight[:, t, :], adj_rows[b][:, t, :], COPY, scale=deg_cols[:, b, t : t + 1])
+            for cols in (slice(0, S2 // 2), slice(S2 // 2, S2)):
+                for t in range(PACK):
+                    nc.scalar.activation(weight[:, t, cols], adj_rows[b][:, t, cols], COPY, scale=deg_cols[:, b, t : t + 1])
             return weight
 
-        def make_h(b, weight, pieces):
-            h_bf16 = sbuf("h_bf16_%d" % b, [P, S2, PACK], BF16)
+        def make_h(b, weight, tags):
+            h_bf16 = [sbuf("h_bf16_%d_%d" % (b, c), [P, J_CHUNK, PACK], BF16, tags.get(c)) for c in range(J_CHUNKS)]
             codes = sbuf("h_codes%d" % b, [P, S2], U32)
             scales = sbuf("h_scales%d" % b, [P, S2], U8)
 
-            def quantise(cols):
+            def quantise(c):
                 nc.vector.quantize_mx(
-                    out=codes[:, cols].bitcast(FP8X4), scales=scales[:, cols], in_=h_bf16[:, cols, :].rearrange("p j t -> p (j t)")
+                    out=codes[:, chunks[c]].bitcast(FP8X4), scales=scales[:, chunks[c]], in_=h_bf16[c][:].rearrange("p j t -> p (j t)")
                 )
 
-            done = 0
             for c, cols in enumerate(chunks):
                 nc.vector.tensor_tensor(
-                    interleaved(h_bf16[:, cols, :], 2), by_rows(compare[(b, c)][:], 2), by_rows(weight[:, :, cols], 2), MULT
+                    interleaved(h_bf16[c][:], 2), by_rows(compare[(b, c)][:], 2), by_rows(weight[:, :, cols], 2), MULT
                 )
-                if pieces[done].stop <= cols.start:
-                    quantise(pieces[done])
-                    done = done + 1
-            for cols in pieces[done:]:
-                quantise(cols)
+                if c > 0:
+                    quantise(c - 1)
+            quantise(J_CHUNKS - 1)
             return codes, scales
 
         whole = [slice(0, S2)]
         chunks = [slice(c * J_CHUNK, (c + 1) * J_CHUNK) for c in range(J_CHUNKS)]
         quantise_wg(*WG_ORDER[0])
-        weights = [weigh_edges(b) for b in range(I_PASSES)]
-        h_mx = [make_h(0, weights[0], whole)]
-        quantise_wg(*WG_ORDER[1])
-        h_mx.append(make_h(1, weights[1], chunks))
-        for b, c in WG_ORDER[2:]:
+        first_weight = weigh_edges(0)
+        h_mx = [make_h(0, first_weight, {})]
+        second_weight = weigh_edges(1)
+        for b, c in WG_ORDER[1:3]:
+            quantise_wg(b, c)
+        h_mx.append(make_h(1, second_weight, {0: "wg_bf16_0_1", 2: "wg_bf16_1_0"}))
+        for b, c in WG_ORDER[3:]:
             quantise_wg(b, c)
 
         def message_pass(n, b, acc, cols):
@@ -247,7 +248,7 @@ def tile_list_gated_graph_messages_kernel(
                 lhsT_scale=msg_scales[:, b, P * n : P * (n + 1)],
                 rhs=h_mx[b][0][:, cols].bitcast(FP8X4),
                 rhs_scale=h_mx[b][1][:, cols],
-                start=(b == 0),
+                start=(b == 0 and cols.start == 0),
                 stop=(b == I_PASSES - 1 and cols.stop == S2),
             )
 
@@ -259,7 +260,7 @@ def tile_list_gated_graph_messages_kernel(
                 lhsT_scale=wg_scales[(b, c)][:, first : first + P],
                 rhs=h_mx[b][0][:, cols].bitcast(FP8X4),
                 rhs_scale=h_mx[b][1][:, cols],
-                start=(b == 0),
+                start=(b == 0 and cols.start == 0),
                 stop=(b == I_PASSES - 1 and cols.stop == S2),
             )
 
@@ -276,14 +277,20 @@ def tile_list_gated_graph_messages_kernel(
             return bank(2 * (n % tiles_at_once) + 1, [P, S2]), bank(2 * (n % tiles_at_once), [P, S2])
 
         accs = [accumulators(n) for n in range(tiles_at_once)]
-        for n, (y_acc, g_acc) in enumerate(accs):
+        first_tiles = list(enumerate(accs))[: J_CHUNKS // 2]
+        for cols in chunks:
+            for n, (y_acc, g_acc) in first_tiles:
+                gate_pass(n, 0, g_acc, cols)
+                message_pass(n, 0, y_acc, cols)
+        for n, (y_acc, g_acc) in list(enumerate(accs))[J_CHUNKS // 2 :]:
             gate_pass(n, 0, g_acc, whole[0])
             message_pass(n, 0, y_acc, whole[0])
-        for cols in chunks:
-            for n, (y_acc, g_acc) in enumerate(accs):
+        for cols in chunks[:-1]:
+            for n, (y_acc, g_acc) in first_tiles:
                 message_pass(n, 1, y_acc, cols)
         for n, (y_acc, g_acc) in enumerate(accs):
             gate_pass(n, 1, g_acc, whole[0])
+            message_pass(n, 1, y_acc, chunks[-1] if n < len(first_tiles) else whole[0])
             finish(n, y_acc, g_acc)
         for n in range(tiles_at_once, N_TILES):
             y_acc, g_acc = accumulators(n)

@@ -55,8 +55,8 @@ def tile_list_gated_graph_messages_kernel(
         identity = tile_in(early, "identity", [P, P], F32)
         bias_rows = tile_in(early, "bias_rows", [P, P], F32)
 
-        def load_table_scales(queue, tile, source):
-            for q in range(QUADRANTS):
+        def load_table_scales(queue, tile, source, quadrants):
+            for q in range(quadrants):
                 queue.dma_start(
                     out=tile[32 * q : 32 * q + SCALE_ROWS * K_PASSES, :].bitcast(I32),
                     in_=source[:, SCALE_ROWS * q : SCALE_ROWS * (q + 1), :].bitcast(I32),
@@ -95,7 +95,7 @@ def tile_list_gated_graph_messages_kernel(
         nc.sync.dma_start(neigh_list[:], offs)
 
         nc.vector.memset(centre_scales[:].bitcast(I32), 0)
-        load_table_scales(nc.scalar, centre_scales, tab2_scales)
+        load_table_scales(nc.scalar, centre_scales, tab2_scales, QUADRANTS)
         with tc.tile_pool(name="first", bufs=1) as first:
             zeros = tile_in(first, "zeros", [P, P], F32)
             nc.vector.memset(zeros[:], 0.0)
@@ -103,7 +103,7 @@ def tile_list_gated_graph_messages_kernel(
                 out=identity[:], in_=zeros[:], compare_op=NOT_EQUAL, fill=1.0, base=0, pattern=[[-1, P]], channel_multiplier=1
             )
         nc.vector.memset(neigh_scales[:].bitcast(I32), 0)
-        load_table_scales(nc.gpsimd, neigh_scales, tab_scales)
+        load_table_scales(nc.gpsimd, neigh_scales, tab_scales, QUADRANTS)
         nc.vector.memset(bias_rows[:], 0.0)
         nc.scalar.dma_start(out=bias_rows[0:N_TILES, :], in_=bg.rearrange("(n p) -> n p", p=P))
 
@@ -117,9 +117,9 @@ def tile_list_gated_graph_messages_kernel(
         neigh_table = [load_words(rest, "neigh_table", tab_words, 0)]
         deg_cols = sbuf("deg_cols", [P, I_PASSES, PACK], F32)
         nc.sync.dma_start(out=deg_cols[:], in_=deg.rearrange("(b p t) -> p b t", p=P, t=PACK))
-        load_wg(0, 0, 1, rest)
         adj_rows = [load_adj(0, rest)]
         neigh_table.extend(load_words(rest, "neigh_table", tab_words, a) for a in range(1, K_PASSES))
+        load_wg(0, 0, 1, rest)
         adj_rows.append(load_adj(1, rest))
         load_msg_scales(nc.sync)
 
@@ -127,9 +127,6 @@ def tile_list_gated_graph_messages_kernel(
         nc.tensor.transpose(bias_turned[:], bias_rows[:], identity[:])
         bias_cols = sbuf("bias_cols", [P, N_TILES], F32)
         nc.scalar.copy(bias_cols[:], bias_turned[:, 0:N_TILES])
-
-        warm = sbuf("warm", [P, 1], F32)
-        nc.scalar.activation(warm[:], deg_cols[:, 0, 0:1], SIGMOID)
 
         centre_words = []
         for a in range(K_PASSES):
@@ -148,23 +145,22 @@ def tile_list_gated_graph_messages_kernel(
         def part_of_list(b):
             return neigh_list[:, b * LIST_COLS : (b + 1) * LIST_COLS]
 
-        def gather_neigh_words(a, b, picked):
-            nc.vector.tensor_copy(picked.rearrange("p t m -> p m t"), neigh_table[a][:].indirect(part_of_list(b)))
+        def gather_dealt(picked, window, b):
+            nc.vector.tensor_copy(picked[:].rearrange("p t m -> p m t"), window[:].indirect(part_of_list(b)))
             return picked
 
-        neigh_words = {}
-        picked_bytes = [sbuf("picked_bytes%d" % b, [P, PASS], U8) for b in range(I_PASSES)]
-        neigh_bytes = [sbuf("neigh_bytes%d" % b, [P, PACK, P], U8) for b in range(I_PASSES)]
+        neigh_words, neigh_bytes = {}, []
         for b in range(I_PASSES):
-            nc.vector.tensor_copy(picked_bytes[b][:], neigh_scales[:].indirect(part_of_list(b)))
-            first_words = sbuf("neigh_words0_%d" % b, [P, PACK, P], U32, tag=(None, "picked_bytes0")[b])
-            neigh_words[(0, b)] = gather_neigh_words(0, b, first_words[:])
-            nc.vector.tensor_copy(neigh_bytes[b][:], picked_bytes[b][:].rearrange("p (m t) -> p t m", t=PACK))
+            neigh_bytes.append(gather_dealt(sbuf("neigh_bytes%d" % b, [P, PACK, P], U8), neigh_scales, b))
+            neigh_words[(0, b)] = gather_dealt(sbuf("neigh_words0_%d" % b, [P, PACK, P], U32), neigh_table[0], b)
         for a in range(1, K_PASSES):
             for b in range(I_PASSES):
-                tag = ("picked_bytes1", "neigh_table0")[b] if a == 1 else None
-                later_words = sbuf("neigh_words%d_%d" % (a, b), [P, PACK, P], U32, tag=tag)
-                neigh_words[(a, b)] = gather_neigh_words(a, b, later_words[:])
+                name = "neigh_words%d_%d" % (a, b)
+                if (a, b) == (1, 0):
+                    later_words = tile_in(early, name, [P, PACK, P], U32, "neigh_scales")
+                else:
+                    later_words = sbuf(name, [P, PACK, P], U32, "neigh_table0" if a == 1 else None)
+                neigh_words[(a, b)] = gather_dealt(later_words, neigh_table[a], b)
             load_wg(a - 1, W_CHUNKS - 1, 1, rest, "neigh_table%d" % a)
 
         compare = {(b, c): bank(b * J_CHUNKS + c, [P, PACK, J_CHUNK]) for b in range(I_PASSES) for c in range(J_CHUNKS)}

@@ -14,9 +14,10 @@ U8 = mybir.dt.uint8
 FP8X4 = mybir.dt.float8_e4m3fn_x4
 FP4X4 = mybir.dt.float4_e2m1fn_x4
 MULT = mybir.AluOpType.mult
+ADD = mybir.AluOpType.add
 NOT_EQUAL = mybir.AluOpType.not_equal
 COPY = mybir.ActivationFunctionType.Copy
-SIGMOID = mybir.ActivationFunctionType.Sigmoid
+TANH = mybir.ActivationFunctionType.Tanh
 
 P = 128
 PACK = 4
@@ -28,11 +29,9 @@ SCALE_ROWS = 4
 J_CHUNK = 128
 J_CHUNKS = S2 // J_CHUNK
 W_CHUNK = 256
-W_CHUNKS = N // W_CHUNK
 N_TILES = N // P
-BANKS = 8
 LIST_COLS = PASS // 16
-WG_ORDER = ((0, 0), (0, 1), (1, 0), (1, 1), (0, 2), (1, 2))
+KIB = 1024
 
 
 def tile_list_gated_graph_messages_kernel(
@@ -42,18 +41,21 @@ def tile_list_gated_graph_messages_kernel(
     with ExitStack() as ctx:
         lists = ctx.enter_context(tc.tile_pool(name="lists", bufs=1))
         early = ctx.enter_context(tc.tile_pool(name="early", bufs=1))
+        placed = ctx.enter_context(tc.tile_pool(name="placed", bufs=1))
         psum = ctx.enter_context(tc.psum_pool(name="psum", bufs=1))
 
         def tile_in(pool, name, shape, dtype, tag=None):
             return pool.tile(shape, dtype, name=name, tag=tag or name, align_bytes=64)
 
+        def tile_at(offset, name, shape, dtype):
+            return placed.tile(shape, dtype, name=name, tag=name, align_bytes=64, offset=offset)
+
         def bank(index, shape):
             return psum.tile(shape, F32, name="bank", tag="bank%d" % index)
 
-        centre_scales = tile_in(early, "centre_scales", [P, T2], U8)
-        neigh_scales = tile_in(early, "neigh_scales", [P, T], U8)
-        identity = tile_in(early, "identity", [P, P], F32)
-        bias_rows = tile_in(early, "bias_rows", [P, P], F32)
+        def load_words(words, source):
+            nc.sync.dma_start(out=words[:].bitcast(I32), in_=source.rearrange("p n t -> p (n t)").bitcast(I32))
+            return words
 
         def load_table_scales(queue, tile, source, quadrants):
             for q in range(quadrants):
@@ -62,106 +64,99 @@ def tile_list_gated_graph_messages_kernel(
                     in_=source[:, SCALE_ROWS * q : SCALE_ROWS * (q + 1), :].bitcast(I32),
                 )
 
-        def load_msg_scales(queue):
-            for q in range(QUADRANTS):
-                queue.dma_start(
-                    out=msg_scales[32 * q : 32 * q + SCALE_ROWS, :, :].bitcast(I32),
-                    in_=m4_scales[:, SCALE_ROWS * q : SCALE_ROWS * (q + 1), :].rearrange("a r n -> r a n").bitcast(I32),
-                )
+        def part_of_list(b):
+            return neigh_list[:, b * LIST_COLS : (b + 1) * LIST_COLS]
 
-        def load_words(pool, name, source, a):
-            words = tile_in(pool, "%s%d" % (name, a), [P, source.shape[2]], U32)
-            nc.sync.dma_start(out=words[:].bitcast(I32), in_=source[a].rearrange("p n t -> p (n t)").bitcast(I32))
-            return words
+        def gather_centres(picked, window):
+            nc.vector.tensor_copy(picked[:], window[:].indirect(centre_list[:]))
+            return picked
 
-        def load_adj(b, pool, tag=None):
-            rows = tile_in(pool, "adj%d" % b, [P, PACK, S2], F32, tag)
-            nc.sync.dma_start(out=rows[:], in_=adj[b * PASS : (b + 1) * PASS, :].rearrange("(p t) j -> p t j", t=PACK))
-            return rows
-
-        wg_rows = {}
-
-        def load_wg(b, first, count, pool, tag=None):
-            rows = tile_in(pool, "wg%d_%d" % (b, first), [P, PACK, count * W_CHUNK], F32, tag)
-            source = wg[b * PASS : (b + 1) * PASS, first * W_CHUNK : (first + count) * W_CHUNK]
-            nc.sync.dma_start(out=rows[:], in_=source.rearrange("(p t) n -> p t n", t=PACK))
-            for c in range(count):
-                wg_rows[(b, first + c)] = rows[:, :, c * W_CHUNK : (c + 1) * W_CHUNK]
+        def gather_dealt(picked, window, b):
+            nc.vector.tensor_copy(picked[:].rearrange("p t m -> p m t"), window[:].indirect(part_of_list(b)))
+            return picked
 
         centre_list = lists.tile([P, S2 // 16], U16, name="centre_list")
         neigh_list = lists.tile([P, S // 16], U16, name="neigh_list")
-        nc.sync.dma_start(centre_list[:], offs2)
-        centre_table = [load_words(early, "centre_table", tab2_words, a) for a in range(K_PASSES)]
-        nc.sync.dma_start(neigh_list[:], offs)
+        neigh_scales = tile_at(13 * KIB, "neigh_scales", [P, T], U8)
+        centre_scales = tile_at(9 * KIB + 512, "centre_scales", [P, T2], U8)
+        msg_scales = tile_in(early, "msg_scales", [P, I_PASSES * N], U8)
+        bias_rows = tile_in(early, "bias_rows", [P, P], F32)
+        zeros = tile_in(early, "zeros", [P, P], F32)
+        identity = tile_in(early, "identity", [P, P], F32)
+        centre_words, neigh_words = {}, {}
+        dealt = [P, PACK, P]
 
-        nc.vector.memset(centre_scales[:].bitcast(I32), 0)
-        load_table_scales(nc.scalar, centre_scales, tab2_scales, QUADRANTS)
-        with tc.tile_pool(name="first", bufs=1) as first:
-            zeros = tile_in(first, "zeros", [P, P], F32)
+        def load_adj(rows, b):
+            nc.sync.dma_start(out=rows[:], in_=adj[b * PASS : (b + 1) * PASS, :].rearrange("(p t) j -> p t j", t=PACK))
+            return rows
+
+        with tc.tile_pool(name="head", bufs=1) as head:
+            nc.sync.dma_start(centre_list[:], offs2)
+            centre_table = [load_words(tile_in(early, "centre_table0", [P, T2], U32), tab2_words[0])]
+            nc.sync.dma_start(neigh_list[:], offs)
+            neigh_table = [load_words(tile_at(0, "neigh_table0", [P, T], U32), tab_words[0])]
+            centre_table.append(load_words(tile_in(head, "centre_table1", [P, T2], U32), tab2_words[1]))
+            neigh_table.append(load_words(tile_in(early, "neigh_table1", [P, T], U32), tab_words[1]))
+            centre_table.append(load_words(tile_in(early, "centre_table2", [P, T2], U32), tab2_words[2]))
+            deg_cols = tile_in(early, "deg_cols", [P, I_PASSES, PACK], F32)
+            nc.sync.dma_start(out=deg_cols[:], in_=deg.rearrange("(b p t) -> p b t", p=P, t=PACK))
+            half_deg = tile_in(early, "half_deg", [P, I_PASSES, PACK], F32)
+            nc.scalar.activation(half_deg[:], deg_cols[:], COPY, scale=0.5)
+
+            nc.vector.memset(neigh_scales[:].bitcast(I32), 0)
+            load_table_scales(nc.gpsimd, neigh_scales, tab_scales, QUADRANTS)
+            nc.vector.memset(centre_scales[:].bitcast(I32), 0)
+            load_table_scales(nc.scalar, centre_scales, tab2_scales, QUADRANTS)
+            nc.vector.memset(bias_rows[:], 0.0)
+            nc.gpsimd.dma_start(out=bias_rows[0:N_TILES, :], in_=bg.rearrange("(n p) -> n p", p=P))
+            nc.vector.memset(msg_scales[:].bitcast(I32), 0)
+            for q in range(QUADRANTS):
+                nc.gpsimd.dma_start(
+                    out=msg_scales[32 * q : 32 * q + SCALE_ROWS, :].rearrange("r (a n) -> r a n", a=I_PASSES).bitcast(I32),
+                    in_=m4_scales[:, SCALE_ROWS * q : SCALE_ROWS * (q + 1), :].rearrange("a r n -> r a n").bitcast(I32),
+                )
             nc.vector.memset(zeros[:], 0.0)
             nc.gpsimd.affine_select(
                 out=identity[:], in_=zeros[:], compare_op=NOT_EQUAL, fill=1.0, base=0, pattern=[[-1, P]], channel_multiplier=1
             )
-        nc.vector.memset(neigh_scales[:].bitcast(I32), 0)
-        load_table_scales(nc.gpsimd, neigh_scales, tab_scales, QUADRANTS)
-        nc.vector.memset(bias_rows[:], 0.0)
-        nc.scalar.dma_start(out=bias_rows[0:N_TILES, :], in_=bg.rearrange("(n p) -> n p", p=P))
+            centre_words[0] = gather_centres(tile_in(early, "centre_words0", [P, S2], U32), centre_table[0])
+            for b in range(I_PASSES):
+                neigh_words[(0, b)] = gather_dealt(tile_in(early, "neigh_words0_%d" % b, dealt, U32), neigh_table[0], b)
+            centre_words[1] = gather_centres(tile_in(early, "centre_words1", [P, S2], U32), centre_table[1])
 
         rest = ctx.enter_context(tc.tile_pool(name="rest", bufs=1))
 
         def sbuf(name, shape, dtype, tag=None):
             return tile_in(rest, name, shape, dtype, tag)
 
-        msg_scales = sbuf("msg_scales", [P, I_PASSES, N], U8)
-        nc.vector.memset(msg_scales[:].bitcast(I32), 0)
-        neigh_table = [load_words(rest, "neigh_table", tab_words, 0)]
-        deg_cols = sbuf("deg_cols", [P, I_PASSES, PACK], F32)
-        nc.sync.dma_start(out=deg_cols[:], in_=deg.rearrange("(b p t) -> p b t", p=P, t=PACK))
-        adj_rows = [load_adj(0, rest)]
-        neigh_table.extend(load_words(rest, "neigh_table", tab_words, a) for a in range(1, K_PASSES))
-        load_wg(0, 0, 1, rest)
-        adj_rows.append(load_adj(1, rest))
-        load_msg_scales(nc.sync)
+        wg_rows = {}
 
-        bias_turned = bank(BANKS - 1, [P, P])
-        nc.tensor.transpose(bias_turned[:], bias_rows[:], identity[:])
-        bias_cols = sbuf("bias_cols", [P, N_TILES], F32)
-        nc.scalar.copy(bias_cols[:], bias_turned[:, 0:N_TILES])
+        def load_wg(b, c):
+            rows = sbuf("wg%d_%d" % (b, c), [P, PACK, W_CHUNK], F32)
+            source = wg[b * PASS : (b + 1) * PASS, c * W_CHUNK : (c + 1) * W_CHUNK]
+            nc.sync.dma_start(out=rows[:], in_=source.rearrange("(p t) n -> p t n", t=PACK))
+            wg_rows[(b, c)] = rows
 
-        centre_words = []
-        for a in range(K_PASSES):
-            picked = sbuf("centre_words%d" % a, [P, S2], U32)
-            nc.vector.tensor_copy(picked[:], centre_table[a][:].indirect(centre_list[:]))
-            centre_words.append(picked)
-        centre_bytes = sbuf("centre_bytes", [P, S2], U8)
-        nc.vector.tensor_copy(centre_bytes[:], centre_scales[:].indirect(centre_list[:]))
-
-        msg_words = tile_in(early, "msg_words", [P, I_PASSES, 2 * N], U8, "centre_table0")
+        adj_rows = [load_adj(sbuf("adj0", [P, PACK, S2], F32), 0)]
+        neigh_table.append(load_words(sbuf("neigh_table2", [P, T], U32), tab_words[2]))
+        load_wg(0, 0)
+        adj_rows.append(load_adj(sbuf("adj1", [P, PACK, S2], F32), 1))
+        load_wg(1, 0)
+        msg_words = sbuf("msg_words", [P, I_PASSES, 2 * N], U8)
         nc.sync.dma_start(out=msg_words[:].bitcast(I32), in_=m4_words.rearrange("a p c -> p a c").bitcast(I32))
-        load_wg(0, 1, 1, early, "centre_table1")
-        load_wg(1, 0, 1, early, "centre_table2")
-        load_wg(1, 1, 1, early, "centre_scales")
-
-        def part_of_list(b):
-            return neigh_list[:, b * LIST_COLS : (b + 1) * LIST_COLS]
-
-        def gather_dealt(picked, window, b):
-            nc.vector.tensor_copy(picked[:].rearrange("p t m -> p m t"), window[:].indirect(part_of_list(b)))
-            return picked
-
-        neigh_words, neigh_bytes = {}, []
-        for b in range(I_PASSES):
-            neigh_bytes.append(gather_dealt(sbuf("neigh_bytes%d" % b, [P, PACK, P], U8), neigh_scales, b))
-            neigh_words[(0, b)] = gather_dealt(sbuf("neigh_words0_%d" % b, [P, PACK, P], U32), neigh_table[0], b)
-        for a in range(1, K_PASSES):
+        for c in (1, 2):
             for b in range(I_PASSES):
-                name = "neigh_words%d_%d" % (a, b)
-                if (a, b) == (1, 0):
-                    later_words = tile_in(early, name, [P, PACK, P], U32, "neigh_scales")
-                else:
-                    later_words = sbuf(name, [P, PACK, P], U32, "neigh_table0" if a == 1 else None)
-                neigh_words[(a, b)] = gather_dealt(later_words, neigh_table[a], b)
-            load_wg(a - 1, W_CHUNKS - 1, 1, rest, "neigh_table%d" % a)
+                load_wg(b, c)
+
+        centre_bytes = gather_centres(tile_at(0, "centre_bytes", [P, S2], U8), centre_scales)
+        neigh_bytes = [
+            gather_dealt(tile_at((b + 1) * PASS, "neigh_bytes%d" % b, dealt, U8), neigh_scales, b) for b in range(I_PASSES)
+        ]
+        neigh_words[(1, 0)] = gather_dealt(tile_at(8 * KIB, "neigh_words1_0", dealt, U32), neigh_table[1], 0)
+        neigh_words[(1, 1)] = gather_dealt(tile_at(12 * KIB, "neigh_words1_1", dealt, U32), neigh_table[1], 1)
+        centre_words[2] = gather_centres(tile_at(10 * KIB, "centre_words2", [P, S2], U32), centre_table[2])
+        neigh_words[(2, 0)] = gather_dealt(tile_at(14 * KIB, "neigh_words2_0", dealt, U32), neigh_table[2], 0)
+        neigh_words[(2, 1)] = gather_dealt(tile_in(early, "neigh_words2_1", dealt, U32, "neigh_table1"), neigh_table[2], 1)
 
         compare = {(b, c): bank(b * J_CHUNKS + c, [P, PACK, J_CHUNK]) for b in range(I_PASSES) for c in range(J_CHUNKS)}
         for a in range(K_PASSES):
@@ -185,113 +180,144 @@ def tile_list_gated_graph_messages_kernel(
         def by_rows(tile, run):
             return tile.rearrange("p t (r i) -> p r t i", i=run)
 
-        wg_codes, wg_scales = {}, {}
+        half = S2 // 2
+        weights = {}
 
-        def quantise_wg(b, c):
-            wg_bf16 = sbuf("wg_bf16_%d_%d" % (b, c), [P, W_CHUNK, PACK], BF16)
-            if (b, c) == WG_ORDER[-1]:
-                nc.vector.tensor_copy(interleaved(wg_bf16[:], 4), by_rows(wg_rows[(b, c)], 4))
-            else:
-                nc.scalar.copy(interleaved(wg_bf16[:], 4), by_rows(wg_rows[(b, c)], 4))
-            codes = sbuf("wg_codes%d_%d" % (b, c), [P, W_CHUNK], U32)
+        def weigh_edges(b):
+            for u in range(2):
+                weight = sbuf("edge_weight%d_%d" % (b, u), [P, PACK, half], F32)
+                for t in range(PACK):
+                    nc.scalar.activation(
+                        weight[:, t, :], adj_rows[b][:, t, u * half : (u + 1) * half], COPY, scale=half_deg[:, b, t : t + 1]
+                    )
+                weights[(b, u)] = weight
+
+        wg_bf16, wg_codes, wg_scales = {}, {}, {}
+
+        def round_wg(copy, b, c, tag=None):
+            rounded = sbuf("wg_bf16_%d_%d" % (b, c), [P, W_CHUNK, PACK], BF16, tag)
+            copy(interleaved(rounded[:], 4), by_rows(wg_rows[(b, c)][:], 4))
+            wg_bf16[(b, c)] = rounded
+
+        def quantise_wg(b, c, tag=None):
+            codes = sbuf("wg_codes%d_%d" % (b, c), [P, W_CHUNK], U32, tag)
             scales = sbuf("wg_scales%d_%d" % (b, c), [P, W_CHUNK], U8)
-            nc.vector.quantize_mx(out=codes[:].bitcast(FP8X4), scales=scales[:], in_=wg_bf16[:].rearrange("p n t -> p (n t)"))
+            nc.vector.quantize_mx(
+                out=codes[:].bitcast(FP8X4), scales=scales[:], in_=wg_bf16[(b, c)][:].rearrange("p n t -> p (n t)")
+            )
             wg_codes[(b, c)] = codes
             wg_scales[(b, c)] = scales
 
-        def weigh_edges(b):
-            weight = sbuf("edge_weight%d" % b, [P, PACK, S2], F32)
-            for cols in (slice(0, S2 // 2), slice(S2 // 2, S2)):
-                for t in range(PACK):
-                    nc.scalar.activation(weight[:, t, cols], adj_rows[b][:, t, cols], COPY, scale=deg_cols[:, b, t : t + 1])
-            return weight
+        h_codes = [sbuf("h_codes%d" % b, [P, S2], U32) for b in range(I_PASSES)]
+        h_scales = [sbuf("h_scales%d" % b, [P, S2], U8) for b in range(I_PASSES)]
+        h_bf16 = {}
 
-        def make_h(b, weight, tags):
-            h_bf16 = [sbuf("h_bf16_%d_%d" % (b, c), [P, J_CHUNK, PACK], BF16, tags.get(c)) for c in range(J_CHUNKS)]
-            codes = sbuf("h_codes%d" % b, [P, S2], U32)
-            scales = sbuf("h_scales%d" % b, [P, S2], U8)
+        def multiply_h(b, c):
+            rounded = sbuf("h_bf16_%d_%d" % (b, c), [P, J_CHUNK, PACK], BF16)
+            u, first = divmod(c * J_CHUNK, half)
+            weight = weights[(b, u)][:, :, first : first + J_CHUNK]
+            nc.vector.tensor_tensor(interleaved(rounded[:], 2), by_rows(compare[(b, c)][:], 2), by_rows(weight, 2), MULT)
+            h_bf16[(b, c)] = rounded
 
-            def quantise(c):
-                nc.vector.quantize_mx(
-                    out=codes[:, chunks[c]].bitcast(FP8X4), scales=scales[:, chunks[c]], in_=h_bf16[c][:].rearrange("p j t -> p (j t)")
-                )
-
-            for c, cols in enumerate(chunks):
-                nc.vector.tensor_tensor(
-                    interleaved(h_bf16[c][:], 2), by_rows(compare[(b, c)][:], 2), by_rows(weight[:, :, cols], 2), MULT
-                )
-                if c > 0:
-                    quantise(c - 1)
-            quantise(J_CHUNKS - 1)
-            return codes, scales
-
-        whole = [slice(0, S2)]
-        chunks = [slice(c * J_CHUNK, (c + 1) * J_CHUNK) for c in range(J_CHUNKS)]
-        quantise_wg(*WG_ORDER[0])
-        first_weight = weigh_edges(0)
-        h_mx = [make_h(0, first_weight, {})]
-        second_weight = weigh_edges(1)
-        for b, c in WG_ORDER[1:3]:
-            quantise_wg(b, c)
-        h_mx.append(make_h(1, second_weight, {0: "wg_bf16_0_1", 2: "wg_bf16_1_0"}))
-        for b, c in WG_ORDER[3:]:
-            quantise_wg(b, c)
-
-        def message_pass(n, b, acc, cols):
-            nc.tensor.matmul_mx(
-                out=acc[:, cols],
-                lhsT=msg_words[:, b, 2 * P * n : 2 * P * (n + 1)].bitcast(FP4X4),
-                lhsT_scale=msg_scales[:, b, P * n : P * (n + 1)],
-                rhs=h_mx[b][0][:, cols].bitcast(FP8X4),
-                rhs_scale=h_mx[b][1][:, cols],
-                start=(b == 0 and cols.start == 0),
-                stop=(b == I_PASSES - 1 and cols.stop == S2),
+        def quantise_h(b, c):
+            cols = slice(c * J_CHUNK, (c + 1) * J_CHUNK)
+            nc.vector.quantize_mx(
+                out=h_codes[b][:, cols].bitcast(FP8X4),
+                scales=h_scales[b][:, cols],
+                in_=h_bf16[(b, c)][:].rearrange("p j t -> p (j t)"),
             )
 
-        def gate_pass(n, b, acc, cols):
+        def make_h(b, between):
+            for c in range(J_CHUNKS):
+                multiply_h(b, c)
+                if c > 0:
+                    quantise_h(b, c - 1)
+            between()
+            quantise_h(b, J_CHUNKS - 1)
+
+        weigh_edges(0)
+        round_wg(nc.scalar.copy, 0, 0)
+        make_h(0, lambda: quantise_wg(0, 0, "edge_weight0_0"))
+        bias_turned = bank(0, [P, P])
+        nc.tensor.transpose(bias_turned[:], bias_rows[:], identity[:])
+        weigh_edges(1)
+        half_bias = sbuf("half_bias", [P, N_TILES], F32, "adj1")
+        nc.scalar.activation(half_bias[:], bias_turned[:, 0:N_TILES], COPY, scale=0.5)
+        round_wg(nc.scalar.copy, 1, 0)
+        make_h(1, lambda: quantise_wg(1, 0))
+
+        def message_pass(n, b):
+            nc.tensor.matmul_mx(
+                out=y_acc[n][:],
+                lhsT=msg_words[:, b, 2 * P * n : 2 * P * (n + 1)].bitcast(FP4X4),
+                lhsT_scale=msg_scales[:, b * N + P * n : b * N + P * (n + 1)],
+                rhs=h_codes[b][:].bitcast(FP8X4),
+                rhs_scale=h_scales[b][:],
+                start=(b == 0),
+                stop=(b == I_PASSES - 1),
+            )
+
+        def gate_pass(n, b):
             c, first = divmod(n * P, W_CHUNK)
             nc.tensor.matmul_mx(
-                out=acc[:, cols],
+                out=g_acc[n][:],
                 lhsT=wg_codes[(b, c)][:, first : first + P].bitcast(FP8X4),
                 lhsT_scale=wg_scales[(b, c)][:, first : first + P],
-                rhs=h_mx[b][0][:, cols].bitcast(FP8X4),
-                rhs_scale=h_mx[b][1][:, cols],
-                start=(b == 0 and cols.start == 0),
-                stop=(b == I_PASSES - 1 and cols.stop == S2),
+                rhs=h_codes[b][:].bitcast(FP8X4),
+                rhs_scale=h_scales[b][:],
+                start=(b == 0),
+                stop=(b == I_PASSES - 1),
             )
 
-        def finish(n, y_acc, g_acc):
-            gate = sbuf("gate%d" % n, [P, S2], F32)
-            nc.scalar.activation(gate[:], g_acc[:], SIGMOID, bias=bias_cols[:, n : n + 1])
-            result = sbuf("result%d" % n, [P, S2], F32)
-            nc.vector.tensor_tensor(result[:], y_acc[:], gate[:], MULT)
-            nc.sync.dma_start(out=out[n * P : (n + 1) * P, :], in_=result[:])
+        def make_gate(n, gate):
+            nc.scalar.activation(gate, g_acc[n][:], TANH, bias=half_bias[:, n : n + 1])
 
-        tiles_at_once = BANKS // 2
+        def finish(n, gate, result):
+            nc.vector.scalar_tensor_tensor(result, gate, 1.0, y_acc[n][:], ADD, MULT)
+            nc.sync.dma_start(out=out[n * P : (n + 1) * P, :], in_=result)
 
-        def accumulators(n):
-            return bank(2 * (n % tiles_at_once) + 1, [P, S2]), bank(2 * (n % tiles_at_once), [P, S2])
-
-        accs = [accumulators(n) for n in range(tiles_at_once)]
-        first_tiles = list(enumerate(accs))[: J_CHUNKS // 2]
-        for cols in chunks:
-            for n, (y_acc, g_acc) in first_tiles:
-                gate_pass(n, 0, g_acc, cols)
-                message_pass(n, 0, y_acc, cols)
-        for n, (y_acc, g_acc) in list(enumerate(accs))[J_CHUNKS // 2 :]:
-            gate_pass(n, 0, g_acc, whole[0])
-            message_pass(n, 0, y_acc, whole[0])
-        for cols in chunks[:-1]:
-            for n, (y_acc, g_acc) in first_tiles:
-                message_pass(n, 1, y_acc, cols)
-        for n, (y_acc, g_acc) in enumerate(accs):
-            gate_pass(n, 1, g_acc, whole[0])
-            message_pass(n, 1, y_acc, chunks[-1] if n < len(first_tiles) else whole[0])
-            finish(n, y_acc, g_acc)
-        for n in range(tiles_at_once, N_TILES):
-            y_acc, g_acc = accumulators(n)
+        whole = [P, S2]
+        pair = [P, 2, S2]
+        g_acc = {0: bank(0, whole), 1: bank(1, whole), 2: bank(6, whole), 3: bank(7, whole)}
+        y_acc = {0: bank(2, whole), 1: bank(3, whole), 2: bank(4, whole), 3: bank(5, whole)}
+        for n in (0, 1):
+            gate_pass(n, 0)
+        for n in (0, 1, 2, 3):
+            message_pass(n, 0)
+        for n in (0, 1):
+            gate_pass(n, 1)
+            message_pass(n, 1)
+        for n in (2, 3):
+            message_pass(n, 1)
+        for b in range(I_PASSES):
+            round_wg(nc.scalar.copy, b, 1)
+            quantise_wg(b, 1)
+            for n in (2, 3):
+                gate_pass(n, b)
+        gates = sbuf("gates0", pair, F32, "wg1_1")
+        results = sbuf("results0", pair, F32)
+        for n in (0, 1):
+            make_gate(n, gates[:, n, :])
+            finish(n, gates[:, n, :], results[:, n, :])
+        round_wg(nc.scalar.copy, 0, 2)
+        round_wg(nc.vector.tensor_copy, 1, 2)
+        quantise_wg(0, 2)
+        quantise_wg(1, 2)
+        for n in (4, 5):
+            g_acc[n] = bank(n - 4, whole)
+            y_acc[n] = bank(n - 2, whole)
             for b in range(I_PASSES):
-                gate_pass(n, b, g_acc, whole[0])
-            for b in range(I_PASSES):
-                message_pass(n, b, y_acc, whole[0])
-            finish(n, y_acc, g_acc)
+                message_pass(n, b)
+        for b in range(I_PASSES):
+            for n in (4, 5):
+                gate_pass(n, b)
+        gates = sbuf("gates1", pair, F32, "wg0_2")
+        results = sbuf("results1", pair, F32, "wg1_2")
+        for n in (2, 3):
+            make_gate(n, gates[:, n - 2, :])
+            finish(n, gates[:, n - 2, :], results[:, n - 2, :])
+        gates = sbuf("gates2", pair, F32)
+        results = sbuf("results2", pair, F32)
+        for n in (4, 5):
+            make_gate(n, gates[:, n - 4, :])
+            finish(n, gates[:, n - 4, :], results[:, n - 4, :])

@@ -1,3 +1,4 @@
+import math
 from contextlib import ExitStack
 
 import concourse.mybir as mybir
@@ -32,6 +33,7 @@ W_CHUNK = 256
 N_TILES = N // P
 LIST_COLS = PASS // 16
 KIB = 1024
+BYTES_OF = {F32: 4, U32: 4, BF16: 2, U8: 1}
 
 
 def tile_list_gated_graph_messages_kernel(
@@ -79,8 +81,6 @@ def tile_list_gated_graph_messages_kernel(
         neigh_list = lists.tile([P, S // 16], U16, name="neigh_list")
         neigh_scales = tile_at(13 * KIB, "neigh_scales", [P, T], U8)
         centre_scales = tile_at(9 * KIB + 512, "centre_scales", [P, T2], U8)
-        msg_scales = tile_in(early, "msg_scales", [P, I_PASSES * N], U8)
-        bias_rows = tile_in(early, "bias_rows", [P, P], F32)
         zeros = tile_in(early, "zeros", [P, P], F32)
         identity = tile_in(early, "identity", [P, P], F32)
         centre_words, neigh_words = {}, {}
@@ -93,70 +93,81 @@ def tile_list_gated_graph_messages_kernel(
         with tc.tile_pool(name="head", bufs=1) as head:
             nc.sync.dma_start(centre_list[:], offs2)
             centre_table = [load_words(tile_in(early, "centre_table0", [P, T2], U32), tab2_words[0])]
+            centre_table.append(load_words(tile_at(31 * KIB, "centre_table1", [P, T2], U32), tab2_words[1]))
             nc.sync.dma_start(neigh_list[:], offs)
-            neigh_table = [load_words(tile_at(0, "neigh_table0", [P, T], U32), tab_words[0])]
-            centre_table.append(load_words(tile_in(head, "centre_table1", [P, T2], U32), tab2_words[1]))
-            neigh_table.append(load_words(tile_in(early, "neigh_table1", [P, T], U32), tab_words[1]))
+            neigh_table = [load_words(tile_in(head, "neigh_table0", [P, T], U32), tab_words[0])]
             centre_table.append(load_words(tile_in(early, "centre_table2", [P, T2], U32), tab2_words[2]))
-            deg_cols = tile_in(early, "deg_cols", [P, I_PASSES, PACK], F32)
-            nc.sync.dma_start(out=deg_cols[:], in_=deg.rearrange("(b p t) -> p b t", p=P, t=PACK))
-            half_deg = tile_in(early, "half_deg", [P, I_PASSES, PACK], F32)
-            nc.scalar.activation(half_deg[:], deg_cols[:], COPY, scale=0.5)
+            neigh_table.append(load_words(tile_at(16 * KIB, "neigh_table1", [P, T], U32), tab_words[1]))
 
             nc.vector.memset(neigh_scales[:].bitcast(I32), 0)
             load_table_scales(nc.gpsimd, neigh_scales, tab_scales, QUADRANTS)
             nc.vector.memset(centre_scales[:].bitcast(I32), 0)
             load_table_scales(nc.scalar, centre_scales, tab2_scales, QUADRANTS)
-            nc.vector.memset(bias_rows[:], 0.0)
-            nc.gpsimd.dma_start(out=bias_rows[0:N_TILES, :], in_=bg.rearrange("(n p) -> n p", p=P))
-            nc.vector.memset(msg_scales[:].bitcast(I32), 0)
-            for q in range(QUADRANTS):
-                nc.gpsimd.dma_start(
-                    out=msg_scales[32 * q : 32 * q + SCALE_ROWS, :].rearrange("r (a n) -> r a n", a=I_PASSES).bitcast(I32),
-                    in_=m4_scales[:, SCALE_ROWS * q : SCALE_ROWS * (q + 1), :].rearrange("a r n -> r a n").bitcast(I32),
-                )
             nc.vector.memset(zeros[:], 0.0)
             nc.gpsimd.affine_select(
                 out=identity[:], in_=zeros[:], compare_op=NOT_EQUAL, fill=1.0, base=0, pattern=[[-1, P]], channel_multiplier=1
             )
-            centre_words[0] = gather_centres(tile_in(early, "centre_words0", [P, S2], U32), centre_table[0])
+            for a in (0, 1):
+                centre_words[a] = gather_centres(tile_in(early, "centre_words%d" % a, [P, S2], U32), centre_table[a])
+
+            deg_cols = tile_at(34 * KIB, "deg_cols", [P, I_PASSES, PACK], F32)
+            nc.sync.dma_start(out=deg_cols[:], in_=deg.rearrange("(b p t) -> p b t", p=P, t=PACK))
+            half_deg = tile_in(early, "half_deg", [P, I_PASSES, PACK], F32)
+            nc.scalar.activation(half_deg[:], deg_cols[:], COPY, scale=0.5)
+            adj_rows = [load_adj(tile_at(24 * KIB, "adj0", [P, PACK, S2], F32), 0)]
+            bias_rows = tile_at(33 * KIB + 512, "bias_rows", [P, P], F32)
+            nc.vector.memset(bias_rows[:], 0.0)
+            nc.sync.dma_start(out=bias_rows[0:N_TILES, :], in_=bg.rearrange("(n p) -> n p", p=P))
+            msg_scales = tile_at(32 * KIB, "msg_scales", [P, I_PASSES * N], U8)
+            nc.vector.memset(msg_scales[:].bitcast(I32), 0)
+            for q in range(QUADRANTS):
+                nc.sync.dma_start(
+                    out=msg_scales[32 * q : 32 * q + SCALE_ROWS, :].rearrange("r (a n) -> r a n", a=I_PASSES).bitcast(I32),
+                    in_=m4_scales[:, SCALE_ROWS * q : SCALE_ROWS * (q + 1), :].rearrange("a r n -> r a n").bitcast(I32),
+                )
             for b in range(I_PASSES):
                 neigh_words[(0, b)] = gather_dealt(tile_in(early, "neigh_words0_%d" % b, dealt, U32), neigh_table[0], b)
-            centre_words[1] = gather_centres(tile_in(early, "centre_words1", [P, S2], U32), centre_table[1])
 
         rest = ctx.enter_context(tc.tile_pool(name="rest", bufs=1))
 
-        def sbuf(name, shape, dtype, tag=None):
-            return tile_in(rest, name, shape, dtype, tag)
+        places = {"free": 0}
+
+        def sbuf(name, shape, dtype, over=None, shift=0):
+            if over is None:
+                places[name] = places["free"]
+                places["free"] = places[name] + max(64, math.prod(shape[1:]) * BYTES_OF[dtype])
+            else:
+                places[name] = places[over] + shift
+            return rest.tile(shape, dtype, name=name, tag=name, align_bytes=64, offset=places[name])
 
         wg_rows = {}
+        piece = [P, PACK, W_CHUNK]
 
-        def load_wg(b, c):
-            rows = sbuf("wg%d_%d" % (b, c), [P, PACK, W_CHUNK], F32)
+        def load_wg(b, c, rows):
             source = wg[b * PASS : (b + 1) * PASS, c * W_CHUNK : (c + 1) * W_CHUNK]
             nc.sync.dma_start(out=rows[:], in_=source.rearrange("(p t) n -> p t n", t=PACK))
             wg_rows[(b, c)] = rows
 
-        adj_rows = [load_adj(sbuf("adj0", [P, PACK, S2], F32), 0)]
         neigh_table.append(load_words(sbuf("neigh_table2", [P, T], U32), tab_words[2]))
-        load_wg(0, 0)
+        load_wg(0, 0, sbuf("wg0_0", piece, F32))
         adj_rows.append(load_adj(sbuf("adj1", [P, PACK, S2], F32), 1))
-        load_wg(1, 0)
+        load_wg(1, 0, sbuf("wg1_0", piece, F32))
         msg_words = sbuf("msg_words", [P, I_PASSES, 2 * N], U8)
         nc.sync.dma_start(out=msg_words[:].bitcast(I32), in_=m4_words.rearrange("a p c -> p a c").bitcast(I32))
-        for c in (1, 2):
-            for b in range(I_PASSES):
-                load_wg(b, c)
+        for b in range(I_PASSES):
+            load_wg(b, 1, tile_at((16 + 4 * b) * KIB, "wg%d_1" % b, piece, F32))
+        for b in range(I_PASSES):
+            load_wg(b, 2, sbuf("wg%d_2" % b, piece, F32, "neigh_table2", 4 * b * KIB))
 
-        centre_bytes = gather_centres(tile_at(0, "centre_bytes", [P, S2], U8), centre_scales)
+        centre_bytes = gather_centres(sbuf("centre_bytes", [P, S2], U8), centre_scales)
         neigh_bytes = [
-            gather_dealt(tile_at((b + 1) * PASS, "neigh_bytes%d" % b, dealt, U8), neigh_scales, b) for b in range(I_PASSES)
+            gather_dealt(sbuf("neigh_bytes%d" % b, dealt, U8), neigh_scales, b) for b in range(I_PASSES)
         ]
         neigh_words[(1, 0)] = gather_dealt(tile_at(8 * KIB, "neigh_words1_0", dealt, U32), neigh_table[1], 0)
         neigh_words[(1, 1)] = gather_dealt(tile_at(12 * KIB, "neigh_words1_1", dealt, U32), neigh_table[1], 1)
         centre_words[2] = gather_centres(tile_at(10 * KIB, "centre_words2", [P, S2], U32), centre_table[2])
         neigh_words[(2, 0)] = gather_dealt(tile_at(14 * KIB, "neigh_words2_0", dealt, U32), neigh_table[2], 0)
-        neigh_words[(2, 1)] = gather_dealt(tile_in(early, "neigh_words2_1", dealt, U32, "neigh_table1"), neigh_table[2], 1)
+        neigh_words[(2, 1)] = gather_dealt(tile_in(early, "neigh_words2_1", dealt, U32, "centre_table2"), neigh_table[2], 1)
 
         compare = {(b, c): bank(b * J_CHUNKS + c, [P, PACK, J_CHUNK]) for b in range(I_PASSES) for c in range(J_CHUNKS)}
         for a in range(K_PASSES):
@@ -294,7 +305,7 @@ def tile_list_gated_graph_messages_kernel(
             quantise_wg(b, 1)
             for n in (2, 3):
                 gate_pass(n, b)
-        gates = sbuf("gates0", pair, F32, "wg1_1")
+        gates = tile_at(20 * KIB, "gates0", pair, F32)
         results = sbuf("results0", pair, F32)
         for n in (0, 1):
             make_gate(n, gates[:, n, :])

@@ -114,7 +114,7 @@ def tile_list_gated_graph_messages_kernel(
             nc.sync.dma_start(out=deg_cols[:], in_=deg.rearrange("(b p t) -> p b t", p=P, t=PACK))
             half_deg = tile_in(early, "half_deg", [P, I_PASSES, PACK], F32)
             nc.scalar.activation(half_deg[:], deg_cols[:], COPY, scale=0.5)
-            adj_rows = [load_adj(tile_at(24 * KIB, "adj0", [P, PACK, S2], F32), 0)]
+            neigh_table.append(load_words(tile_at(24 * KIB, "neigh_table2", [P, T], U32), tab_words[2]))
             bias_rows = tile_at(33 * KIB + 512, "bias_rows", [P, P], F32)
             nc.vector.memset(bias_rows[:], 0.0)
             nc.sync.dma_start(out=bias_rows[0:N_TILES, :], in_=bg.rearrange("(n p) -> n p", p=P))
@@ -148,16 +148,15 @@ def tile_list_gated_graph_messages_kernel(
             nc.sync.dma_start(out=rows[:], in_=source.rearrange("(p t) n -> p t n", t=PACK))
             wg_rows[(b, c)] = rows
 
-        neigh_table.append(load_words(sbuf("neigh_table2", [P, T], U32), tab_words[2]))
+        adj_rows = [load_adj(sbuf("adj0", [P, PACK, S2], F32), 0)]
         load_wg(0, 0, sbuf("wg0_0", piece, F32))
         adj_rows.append(load_adj(sbuf("adj1", [P, PACK, S2], F32), 1))
         load_wg(1, 0, sbuf("wg1_0", piece, F32))
         msg_words = sbuf("msg_words", [P, I_PASSES, 2 * N], U8)
         nc.sync.dma_start(out=msg_words[:].bitcast(I32), in_=m4_words.rearrange("a p c -> p a c").bitcast(I32))
-        for b in range(I_PASSES):
-            load_wg(b, 1, tile_at((16 + 4 * b) * KIB, "wg%d_1" % b, piece, F32))
-        for b in range(I_PASSES):
-            load_wg(b, 2, sbuf("wg%d_2" % b, piece, F32, "neigh_table2", 4 * b * KIB))
+        for c in (1, 2):
+            for b in range(I_PASSES):
+                load_wg(b, c, tile_at((8 + 8 * c + 4 * b) * KIB, "wg%d_%d" % (b, c), piece, F32))
 
         centre_bytes = gather_centres(sbuf("centre_bytes", [P, S2], U8), centre_scales)
         neigh_bytes = [
@@ -257,27 +256,27 @@ def tile_list_gated_graph_messages_kernel(
         round_wg(nc.scalar.copy, 1, 0)
         make_h(1, lambda: quantise_wg(1, 0))
 
-        def message_pass(n, b):
+        def message_pass(n, b, cols=slice(0, S2)):
             nc.tensor.matmul_mx(
-                out=y_acc[n][:],
+                out=y_acc[n][:, cols],
                 lhsT=msg_words[:, b, 2 * P * n : 2 * P * (n + 1)].bitcast(FP4X4),
                 lhsT_scale=msg_scales[:, b * N + P * n : b * N + P * (n + 1)],
-                rhs=h_codes[b][:].bitcast(FP8X4),
-                rhs_scale=h_scales[b][:],
+                rhs=h_codes[b][:, cols].bitcast(FP8X4),
+                rhs_scale=h_scales[b][:, cols],
                 start=(b == 0),
-                stop=(b == I_PASSES - 1),
+                stop=(b == I_PASSES - 1 and cols.stop == S2),
             )
 
-        def gate_pass(n, b):
+        def gate_pass(n, b, cols=slice(0, S2)):
             c, first = divmod(n * P, W_CHUNK)
             nc.tensor.matmul_mx(
-                out=g_acc[n][:],
+                out=g_acc[n][:, cols],
                 lhsT=wg_codes[(b, c)][:, first : first + P].bitcast(FP8X4),
                 lhsT_scale=wg_scales[(b, c)][:, first : first + P],
-                rhs=h_codes[b][:].bitcast(FP8X4),
-                rhs_scale=h_scales[b][:],
+                rhs=h_codes[b][:, cols].bitcast(FP8X4),
+                rhs_scale=h_scales[b][:, cols],
                 start=(b == 0),
-                stop=(b == I_PASSES - 1),
+                stop=(b == I_PASSES - 1 and cols.stop == S2),
             )
 
         def make_gate(n, gate):
@@ -295,11 +294,14 @@ def tile_list_gated_graph_messages_kernel(
             gate_pass(n, 0)
         for n in (0, 1, 2, 3):
             message_pass(n, 0)
-        for n in (0, 1):
-            gate_pass(n, 1)
-            message_pass(n, 1)
-        for n in (2, 3):
-            message_pass(n, 1)
+        first_half, second_half = slice(0, half), slice(half, S2)
+        for n in (0, 1, 2, 3):
+            message_pass(n, 1, first_half)
+        for cols in (first_half, second_half):
+            for n in (0, 1):
+                gate_pass(n, 1, cols)
+        for n in (0, 1, 2, 3):
+            message_pass(n, 1, second_half)
         for b in range(I_PASSES):
             round_wg(nc.scalar.copy, b, 1)
             quantise_wg(b, 1)
@@ -314,19 +316,22 @@ def tile_list_gated_graph_messages_kernel(
         round_wg(nc.vector.tensor_copy, 1, 2)
         quantise_wg(0, 2)
         quantise_wg(1, 2)
+        y_acc[4] = bank(2, whole)
+        for b in range(I_PASSES):
+            message_pass(4, b)
         for n in (4, 5):
             g_acc[n] = bank(n - 4, whole)
-            y_acc[n] = bank(n - 2, whole)
-            for b in range(I_PASSES):
-                message_pass(n, b)
         for b in range(I_PASSES):
             for n in (4, 5):
                 gate_pass(n, b)
-        gates = sbuf("gates1", pair, F32, "wg0_2")
-        results = sbuf("results1", pair, F32, "wg1_2")
+        gates = tile_at(24 * KIB, "gates1", pair, F32)
+        results = tile_at(28 * KIB, "results1", pair, F32)
         for n in (2, 3):
             make_gate(n, gates[:, n - 2, :])
             finish(n, gates[:, n - 2, :], results[:, n - 2, :])
+        y_acc[5] = bank(4, whole)
+        for b in range(I_PASSES):
+            message_pass(5, b)
         gates = sbuf("gates2", pair, F32)
         results = sbuf("results2", pair, F32)
         for n in (4, 5):

@@ -115,6 +115,7 @@ def tile_list_gated_graph_messages_kernel(
             half_deg = tile_in(early, "half_deg", [P, I_PASSES, PACK], F32)
             nc.scalar.activation(half_deg[:], deg_cols[:], COPY, scale=0.5)
             neigh_table.append(load_words(tile_at(24 * KIB, "neigh_table2", [P, T], U32), tab_words[2]))
+            adj_rows = [load_adj(tile_at(34 * KIB + 512, "adj0", [P, PACK, S2], F32), 0)]
             bias_rows = tile_at(33 * KIB + 512, "bias_rows", [P, P], F32)
             nc.vector.memset(bias_rows[:], 0.0)
             nc.sync.dma_start(out=bias_rows[0:N_TILES, :], in_=bg.rearrange("(n p) -> n p", p=P))
@@ -148,7 +149,6 @@ def tile_list_gated_graph_messages_kernel(
             nc.sync.dma_start(out=rows[:], in_=source.rearrange("(p t) n -> p t n", t=PACK))
             wg_rows[(b, c)] = rows
 
-        adj_rows = [load_adj(sbuf("adj0", [P, PACK, S2], F32), 0)]
         load_wg(0, 0, sbuf("wg0_0", piece, F32))
         adj_rows.append(load_adj(sbuf("adj1", [P, PACK, S2], F32), 1))
         load_wg(1, 0, sbuf("wg1_0", piece, F32))
@@ -204,19 +204,23 @@ def tile_list_gated_graph_messages_kernel(
 
         wg_bf16, wg_codes, wg_scales = {}, {}, {}
 
-        def round_wg(copy, b, c, tag=None):
-            rounded = sbuf("wg_bf16_%d_%d" % (b, c), [P, W_CHUNK, PACK], BF16, tag)
-            copy(interleaved(rounded[:], 4), by_rows(wg_rows[(b, c)][:], 4))
-            wg_bf16[(b, c)] = rounded
+        def round_wg(copy, b, tiles, over=None, shift=0):
+            c, first = divmod(tiles[0] * P, W_CHUNK)
+            width = len(tiles) * P
+            rounded = sbuf("wg_bf16_%d_%d" % (b, tiles[0]), [P, width, PACK], BF16, over, shift)
+            copy(interleaved(rounded[:], 4), by_rows(wg_rows[(b, c)][:, :, first : first + width], 4))
+            wg_bf16[(b, tiles)] = rounded
 
-        def quantise_wg(b, c, tag=None):
-            codes = sbuf("wg_codes%d_%d" % (b, c), [P, W_CHUNK], U32, tag)
-            scales = sbuf("wg_scales%d_%d" % (b, c), [P, W_CHUNK], U8)
+        def quantise_wg(b, tiles, over=None, shift=0):
+            width = len(tiles) * P
+            codes = sbuf("wg_codes%d_%d" % (b, tiles[0]), [P, width], U32)
+            scales = sbuf("wg_scales%d_%d" % (b, tiles[0]), [P, width], U8, over, shift)
             nc.vector.quantize_mx(
-                out=codes[:].bitcast(FP8X4), scales=scales[:], in_=wg_bf16[(b, c)][:].rearrange("p n t -> p (n t)")
+                out=codes[:].bitcast(FP8X4), scales=scales[:], in_=wg_bf16[(b, tiles)][:].rearrange("p n t -> p (n t)")
             )
-            wg_codes[(b, c)] = codes
-            wg_scales[(b, c)] = scales
+            for place, n in enumerate(tiles):
+                wg_codes[(b, n)] = codes[:, place * P : (place + 1) * P]
+                wg_scales[(b, n)] = scales[:, place * P : (place + 1) * P]
 
         h_codes = [sbuf("h_codes%d" % b, [P, S2], U32) for b in range(I_PASSES)]
         h_scales = [sbuf("h_scales%d" % b, [P, S2], U8) for b in range(I_PASSES)]
@@ -246,15 +250,15 @@ def tile_list_gated_graph_messages_kernel(
             quantise_h(b, J_CHUNKS - 1)
 
         weigh_edges(0)
-        round_wg(nc.scalar.copy, 0, 0)
-        make_h(0, lambda: quantise_wg(0, 0, "edge_weight0_0"))
+        round_wg(nc.scalar.copy, 0, (0, 1))
+        make_h(0, lambda: quantise_wg(0, (0, 1), "edge_weight0_0"))
         bias_turned = bank(0, [P, P])
         nc.tensor.transpose(bias_turned[:], bias_rows[:], identity[:])
         weigh_edges(1)
         half_bias = sbuf("half_bias", [P, N_TILES], F32, "adj1")
         nc.scalar.activation(half_bias[:], bias_turned[:, 0:N_TILES], COPY, scale=0.5)
-        round_wg(nc.scalar.copy, 1, 0)
-        make_h(1, lambda: quantise_wg(1, 0))
+        round_wg(nc.scalar.copy, 1, (0, 1))
+        make_h(1, lambda: quantise_wg(1, (0, 1)))
 
         def message_pass(n, b, cols=slice(0, S2)):
             nc.tensor.matmul_mx(
@@ -268,23 +272,22 @@ def tile_list_gated_graph_messages_kernel(
             )
 
         def gate_pass(n, b, cols=slice(0, S2)):
-            c, first = divmod(n * P, W_CHUNK)
             nc.tensor.matmul_mx(
                 out=g_acc[n][:, cols],
-                lhsT=wg_codes[(b, c)][:, first : first + P].bitcast(FP8X4),
-                lhsT_scale=wg_scales[(b, c)][:, first : first + P],
+                lhsT=wg_codes[(b, n)].bitcast(FP8X4),
+                lhsT_scale=wg_scales[(b, n)],
                 rhs=h_codes[b][:, cols].bitcast(FP8X4),
                 rhs_scale=h_scales[b][:, cols],
                 start=(b == 0),
                 stop=(b == I_PASSES - 1 and cols.stop == S2),
             )
 
-        def make_gate(n, gate):
-            nc.scalar.activation(gate, g_acc[n][:], TANH, bias=half_bias[:, n : n + 1])
+        def make_gate(n, gate, cols=slice(0, S2)):
+            nc.scalar.activation(gate, g_acc[n][:, cols], TANH, bias=half_bias[:, n : n + 1])
 
-        def finish(n, gate, result):
-            nc.vector.scalar_tensor_tensor(result, gate, 1.0, y_acc[n][:], ADD, MULT)
-            nc.sync.dma_start(out=out[n * P : (n + 1) * P, :], in_=result)
+        def finish(n, gate, result, cols=slice(0, S2)):
+            nc.vector.scalar_tensor_tensor(result, gate, 1.0, y_acc[n][:, cols], ADD, MULT)
+            nc.sync.dma_start(out=out[n * P : (n + 1) * P, cols], in_=result)
 
         whole = [P, S2]
         pair = [P, 2, S2]
@@ -303,8 +306,8 @@ def tile_list_gated_graph_messages_kernel(
         for n in (0, 1, 2, 3):
             message_pass(n, 1, second_half)
         for b in range(I_PASSES):
-            round_wg(nc.scalar.copy, b, 1)
-            quantise_wg(b, 1)
+            round_wg(nc.scalar.copy, b, (2, 3))
+            quantise_wg(b, (2, 3))
             for n in (2, 3):
                 gate_pass(n, b)
         gates = tile_at(20 * KIB, "gates0", pair, F32)
@@ -312,10 +315,12 @@ def tile_list_gated_graph_messages_kernel(
         for n in (0, 1):
             make_gate(n, gates[:, n, :])
             finish(n, gates[:, n, :], results[:, n, :])
-        round_wg(nc.scalar.copy, 0, 2)
-        round_wg(nc.vector.tensor_copy, 1, 2)
-        quantise_wg(0, 2)
-        quantise_wg(1, 2)
+        round_wg(nc.scalar.copy, 0, (4, 5))
+        for n in (4, 5):
+            round_wg(nc.vector.tensor_copy, 1, (n,))
+        quantise_wg(0, (4, 5))
+        for n in (4, 5):
+            quantise_wg(1, (n,))
         y_acc[4] = bank(2, whole)
         for b in range(I_PASSES):
             message_pass(4, b)
@@ -334,6 +339,6 @@ def tile_list_gated_graph_messages_kernel(
             message_pass(5, b)
         gates = sbuf("gates2", pair, F32)
         results = sbuf("results2", pair, F32)
-        for n in (4, 5):
-            make_gate(n, gates[:, n - 4, :])
-            finish(n, gates[:, n - 4, :], results[:, n - 4, :])
+        for n, cols in ((4, slice(0, S2)), (5, first_half), (5, second_half)):
+            make_gate(n, gates[:, n - 4, cols], cols)
+            finish(n, gates[:, n - 4, cols], results[:, n - 4, cols], cols)

@@ -145,18 +145,28 @@ def tile_list_gated_graph_messages_kernel(
         piece = [P, PACK, W_CHUNK]
 
         def load_wg(b, c, rows):
-            source = wg[b * PASS : (b + 1) * PASS, c * W_CHUNK : (c + 1) * W_CHUNK]
+            width = rows.shape[2]
+            source = wg[b * PASS : (b + 1) * PASS, c * W_CHUNK : c * W_CHUNK + width]
             nc.sync.dma_start(out=rows[:], in_=source.rearrange("(p t) n -> p t n", t=PACK))
-            wg_rows[(b, c)] = rows
+            for k in range(width // W_CHUNK):
+                wg_rows[(b, c + k)] = rows[:, :, k * W_CHUNK : (k + 1) * W_CHUNK]
 
-        load_wg(0, 0, sbuf("wg0_0", piece, F32))
+        msg_words = {}
+
+        def load_messages(tiles, words):
+            source = m4_words[:, :, 2 * P * tiles[0] : 2 * P * (tiles[-1] + 1)]
+            nc.sync.dma_start(out=words[:].bitcast(I32), in_=source.rearrange("a p c -> p a c").bitcast(I32))
+            for place, n in enumerate(tiles):
+                msg_words[n] = words[:, :, 2 * P * place : 2 * P * (place + 1)]
+
+        load_wg(0, 0, sbuf("wg0_0", [P, PACK, 2 * W_CHUNK], F32))
         adj_rows.append(load_adj(sbuf("adj1", [P, PACK, S2], F32), 1))
         load_wg(1, 0, sbuf("wg1_0", piece, F32))
-        msg_words = sbuf("msg_words", [P, I_PASSES, 2 * N], U8)
-        nc.sync.dma_start(out=msg_words[:].bitcast(I32), in_=m4_words.rearrange("a p c -> p a c").bitcast(I32))
-        for c in (1, 2):
-            for b in range(I_PASSES):
-                load_wg(b, c, tile_at((8 + 8 * c + 4 * b) * KIB, "wg%d_%d" % (b, c), piece, F32))
+        load_messages((0, 1, 2, 3), sbuf("first_messages", [P, I_PASSES, 8 * P], U8))
+        load_wg(1, 1, tile_at(16 * KIB, "wg1_1", piece, F32))
+        for b in range(I_PASSES):
+            load_wg(b, 2, tile_at((23 + 4 * b) * KIB, "wg%d_2" % b, piece, F32))
+        load_messages((4, 5), tile_at(31 * KIB, "last_messages", [P, I_PASSES, 4 * P], U8))
 
         centre_bytes = gather_centres(sbuf("centre_bytes", [P, S2], U8), centre_scales)
         neigh_bytes = [
@@ -251,7 +261,9 @@ def tile_list_gated_graph_messages_kernel(
 
         weigh_edges(0)
         round_wg(nc.scalar.copy, 0, (0, 1))
+        round_wg(nc.scalar.copy, 0, (2, 3))
         make_h(0, lambda: quantise_wg(0, (0, 1), "edge_weight0_0"))
+        quantise_wg(0, (2, 3), "h_bf16_0_2")
         bias_turned = bank(0, [P, P])
         nc.tensor.transpose(bias_turned[:], bias_rows[:], identity[:])
         weigh_edges(1)
@@ -263,7 +275,7 @@ def tile_list_gated_graph_messages_kernel(
         def message_pass(n, b, cols=slice(0, S2)):
             nc.tensor.matmul_mx(
                 out=y_acc[n][:, cols],
-                lhsT=msg_words[:, b, 2 * P * n : 2 * P * (n + 1)].bitcast(FP4X4),
+                lhsT=msg_words[n][:, b, :].bitcast(FP4X4),
                 lhsT_scale=msg_scales[:, b * N + P * n : b * N + P * (n + 1)],
                 rhs=h_codes[b][:, cols].bitcast(FP8X4),
                 rhs_scale=h_scales[b][:, cols],
@@ -305,12 +317,12 @@ def tile_list_gated_graph_messages_kernel(
                 gate_pass(n, 1, cols)
         for n in (0, 1, 2, 3):
             message_pass(n, 1, second_half)
+        round_wg(nc.scalar.copy, 1, (2, 3))
+        quantise_wg(1, (2, 3))
         for b in range(I_PASSES):
-            round_wg(nc.scalar.copy, b, (2, 3))
-            quantise_wg(b, (2, 3))
             for n in (2, 3):
                 gate_pass(n, b)
-        gates = tile_at(20 * KIB, "gates0", pair, F32)
+        gates = tile_at(16 * KIB, "gates0", pair, F32)
         results = sbuf("results0", pair, F32)
         for n in (0, 1):
             make_gate(n, gates[:, n, :])
@@ -329,8 +341,8 @@ def tile_list_gated_graph_messages_kernel(
         for b in range(I_PASSES):
             for n in (4, 5):
                 gate_pass(n, b)
-        gates = tile_at(24 * KIB, "gates1", pair, F32)
-        results = tile_at(28 * KIB, "results1", pair, F32)
+        gates = tile_at(23 * KIB, "gates1", pair, F32)
+        results = tile_at(27 * KIB, "results1", pair, F32)
         for n in (2, 3):
             make_gate(n, gates[:, n - 2, :])
             finish(n, gates[:, n - 2, :], results[:, n - 2, :])

@@ -96,7 +96,7 @@ def tile_list_gated_graph_messages_kernel(
             centre_table.append(load_words(tile_at(31 * KIB, "centre_table1", [P, T2], U32), tab2_words[1]))
             nc.sync.dma_start(neigh_list[:], offs)
             neigh_table = [load_words(tile_in(head, "neigh_table0", [P, T], U32), tab_words[0])]
-            centre_table.append(load_words(tile_in(early, "centre_table2", [P, T2], U32), tab2_words[2]))
+            centre_table.append(load_words(tile_at(0, "centre_table2", [P, T2], U32), tab2_words[2]))
             neigh_table.append(load_words(tile_at(16 * KIB, "neigh_table1", [P, T], U32), tab_words[1]))
 
             nc.vector.memset(neigh_scales[:].bitcast(I32), 0)
@@ -163,36 +163,38 @@ def tile_list_gated_graph_messages_kernel(
         adj_rows.append(load_adj(sbuf("adj1", [P, PACK, S2], F32), 1))
         load_wg(1, 0, sbuf("wg1_0", piece, F32))
         load_messages((0, 1, 2, 3), sbuf("first_messages", [P, I_PASSES, 8 * P], U8))
+
+        centre_words[2] = gather_centres(tile_in(early, "centre_words2", [P, S2], U32), centre_table[2])
+        centre_bytes = gather_centres(tile_at(0, "centre_bytes", [P, S2], U8), centre_scales)
+        neigh_bytes = [
+            gather_dealt(tile_at((b + 1) * PASS, "neigh_bytes%d" % b, dealt, U8), neigh_scales, b) for b in range(I_PASSES)
+        ]
+        neigh_words[(1, 0)] = gather_dealt(tile_at(8 * KIB, "neigh_words1_0", dealt, U32), neigh_table[1], 0)
+        neigh_words[(2, 0)] = gather_dealt(tile_at(14 * KIB, "neigh_words2_0", dealt, U32), neigh_table[2], 0)
+        neigh_words[(2, 1)] = gather_dealt(tile_at(2 * KIB, "neigh_words2_1", dealt, U32), neigh_table[2], 1)
+        neigh_words[(1, 1)] = gather_dealt(tile_at(29 * KIB, "neigh_words1_1", dealt, U32), neigh_table[1], 1)
+
+        compare = {(b, c): bank(b * J_CHUNKS + c, [P, PACK, J_CHUNK]) for b in range(I_PASSES) for c in range(J_CHUNKS)}
+        steps = ((0, 0), (0, 1), (1, 0), (2, 0), (2, 1), (1, 1))
+        for a, b in steps:
+            last = [step for step in steps if step[1] == b][-1]
+            for c in range(J_CHUNKS):
+                cols = slice(c * J_CHUNK, (c + 1) * J_CHUNK)
+                for t in range(PACK):
+                    nc.tensor.matmul_mx(
+                        out=compare[(b, c)][:, t, :],
+                        lhsT=neigh_words[(a, b)][:, t, :].bitcast(FP8X4),
+                        lhsT_scale=neigh_bytes[b][SCALE_ROWS * a :, t, :],
+                        rhs=centre_words[a][:, cols].bitcast(FP8X4),
+                        rhs_scale=centre_bytes[SCALE_ROWS * a :, cols],
+                        start=(a == 0 and t == 0),
+                        stop=((a, b) == last and t == PACK - 1),
+                    )
+
         load_wg(1, 1, tile_at(16 * KIB, "wg1_1", piece, F32))
         for b in range(I_PASSES):
             load_wg(b, 2, tile_at((23 + 4 * b) * KIB, "wg%d_2" % b, piece, F32))
         load_messages((4, 5), tile_at(31 * KIB, "last_messages", [P, I_PASSES, 4 * P], U8))
-
-        centre_bytes = gather_centres(sbuf("centre_bytes", [P, S2], U8), centre_scales)
-        neigh_bytes = [
-            gather_dealt(sbuf("neigh_bytes%d" % b, dealt, U8), neigh_scales, b) for b in range(I_PASSES)
-        ]
-        neigh_words[(1, 0)] = gather_dealt(tile_at(8 * KIB, "neigh_words1_0", dealt, U32), neigh_table[1], 0)
-        neigh_words[(1, 1)] = gather_dealt(tile_at(12 * KIB, "neigh_words1_1", dealt, U32), neigh_table[1], 1)
-        centre_words[2] = gather_centres(tile_at(10 * KIB, "centre_words2", [P, S2], U32), centre_table[2])
-        neigh_words[(2, 0)] = gather_dealt(tile_at(14 * KIB, "neigh_words2_0", dealt, U32), neigh_table[2], 0)
-        neigh_words[(2, 1)] = gather_dealt(tile_in(early, "neigh_words2_1", dealt, U32, "centre_table2"), neigh_table[2], 1)
-
-        compare = {(b, c): bank(b * J_CHUNKS + c, [P, PACK, J_CHUNK]) for b in range(I_PASSES) for c in range(J_CHUNKS)}
-        for a in range(K_PASSES):
-            for b in range(I_PASSES):
-                for c in range(J_CHUNKS):
-                    cols = slice(c * J_CHUNK, (c + 1) * J_CHUNK)
-                    for t in range(PACK):
-                        nc.tensor.matmul_mx(
-                            out=compare[(b, c)][:, t, :],
-                            lhsT=neigh_words[(a, b)][:, t, :].bitcast(FP8X4),
-                            lhsT_scale=neigh_bytes[b][SCALE_ROWS * a :, t, :],
-                            rhs=centre_words[a][:, cols].bitcast(FP8X4),
-                            rhs_scale=centre_bytes[SCALE_ROWS * a :, cols],
-                            start=(a == 0 and t == 0),
-                            stop=(a == K_PASSES - 1 and t == PACK - 1),
-                        )
 
         def interleaved(tile, run):
             return tile.rearrange("p (r i) t -> p r t i", i=run)
@@ -318,7 +320,7 @@ def tile_list_gated_graph_messages_kernel(
         for n in (0, 1, 2, 3):
             message_pass(n, 1, second_half)
         round_wg(nc.scalar.copy, 1, (2, 3))
-        quantise_wg(1, (2, 3))
+        quantise_wg(1, (2, 3), "h_bf16_1_2")
         for b in range(I_PASSES):
             for n in (2, 3):
                 gate_pass(n, b)
@@ -328,9 +330,9 @@ def tile_list_gated_graph_messages_kernel(
             make_gate(n, gates[:, n, :])
             finish(n, gates[:, n, :], results[:, n, :])
         round_wg(nc.scalar.copy, 0, (4, 5))
+        quantise_wg(0, (4, 5), "h_bf16_1_3")
         for n in (4, 5):
-            round_wg(nc.vector.tensor_copy, 1, (n,))
-        quantise_wg(0, (4, 5))
+            round_wg(nc.vector.tensor_copy, 1, (n,), "wg_bf16_1_2", (n - 4) * KIB)
         for n in (4, 5):
             quantise_wg(1, (n,))
         y_acc[4] = bank(2, whole)

@@ -97,7 +97,7 @@ def tile_list_gated_graph_messages_kernel(
             nc.sync.dma_start(neigh_list[:], offs)
             neigh_table = [load_words(tile_in(head, "neigh_table0", [P, T], U32), tab_words[0])]
             centre_table.append(load_words(tile_at(0, "centre_table2", [P, T2], U32), tab2_words[2]))
-            neigh_table.append(load_words(tile_at(16 * KIB, "neigh_table1", [P, T], U32), tab_words[1]))
+            neigh_table.append(load_words(tile_in(early, "neigh_table1", [P, T], U32), tab_words[1]))
 
             nc.vector.memset(neigh_scales[:].bitcast(I32), 0)
             load_table_scales(nc.gpsimd, neigh_scales, tab_scales, QUADRANTS)
@@ -161,7 +161,7 @@ def tile_list_gated_graph_messages_kernel(
 
         load_wg(0, 0, sbuf("wg0_0", [P, PACK, 2 * W_CHUNK], F32))
         adj_rows.append(load_adj(sbuf("adj1", [P, PACK, S2], F32), 1))
-        load_wg(1, 0, sbuf("wg1_0", piece, F32))
+        load_wg(1, 0, sbuf("wg1_0", [P, PACK, 2 * W_CHUNK], F32))
         load_messages((0, 1, 2, 3), sbuf("first_messages", [P, I_PASSES, 8 * P], U8))
 
         centre_words[2] = gather_centres(tile_in(early, "centre_words2", [P, S2], U32), centre_table[2])
@@ -191,7 +191,6 @@ def tile_list_gated_graph_messages_kernel(
                         stop=((a, b) == last and t == PACK - 1),
                     )
 
-        load_wg(1, 1, tile_at(16 * KIB, "wg1_1", piece, F32))
         for b in range(I_PASSES):
             load_wg(b, 2, tile_at((23 + 4 * b) * KIB, "wg%d_2" % b, piece, F32))
         load_messages((4, 5), tile_at(31 * KIB, "last_messages", [P, I_PASSES, 4 * P], U8))
@@ -324,7 +323,7 @@ def tile_list_gated_graph_messages_kernel(
         for b in range(I_PASSES):
             for n in (2, 3):
                 gate_pass(n, b)
-        gates = tile_at(16 * KIB, "gates0", pair, F32)
+        gates = sbuf("gates0", pair, F32, "wg1_0")
         results = sbuf("results0", pair, F32)
         for n in (0, 1):
             make_gate(n, gates[:, n, :])

import math
from contextlib import ExitStack

import concourse.mybir as mybir

K, T, S, T2, S2, N = 1536, 2048, 1024, 1024, 512, 768
FLOPS = 2 * K * S * S2 + 2 * 2 * S * N * S2

F32 = mybir.dt.float32
BF16 = mybir.dt.bfloat16
I32 = mybir.dt.int32
U32 = mybir.dt.uint32
U16 = mybir.dt.uint16
U8 = mybir.dt.uint8
FP8X4 = mybir.dt.float8_e4m3fn_x4
FP4X4 = mybir.dt.float4_e2m1fn_x4
MULT = mybir.AluOpType.mult
ADD = mybir.AluOpType.add
NOT_EQUAL = mybir.AluOpType.not_equal
COPY = mybir.ActivationFunctionType.Copy
TANH = mybir.ActivationFunctionType.Tanh

P = 128
PACK = 4
PASS = P * PACK
K_PASSES = K // PASS
I_PASSES = S // PASS
QUADRANTS = 4
SCALE_ROWS = 4
J_CHUNK = 128
J_CHUNKS = S2 // J_CHUNK
W_CHUNK = 256
N_TILES = N // P
LIST_COLS = PASS // 16
KIB = 1024
BYTES_OF = {F32: 4, U32: 4, BF16: 2, U8: 1}


def tile_list_gated_graph_messages_kernel(
    tc, tab_words, tab_scales, tab2_words, tab2_scales, offs, offs2, adj, deg, m4_words, m4_scales, wg, bg, out
):
    nc = tc.nc
    with ExitStack() as ctx:
        lists = ctx.enter_context(tc.tile_pool(name="lists", bufs=1))
        early = ctx.enter_context(tc.tile_pool(name="early", bufs=1))
        placed = ctx.enter_context(tc.tile_pool(name="placed", bufs=1))
        psum = ctx.enter_context(tc.psum_pool(name="psum", bufs=1))

        def tile_in(pool, name, shape, dtype, tag=None):
            return pool.tile(shape, dtype, name=name, tag=tag or name, align_bytes=64)

        def tile_at(offset, name, shape, dtype):
            return placed.tile(shape, dtype, name=name, tag=name, align_bytes=64, offset=offset)

        def bank(index, shape):
            return psum.tile(shape, F32, name="bank", tag="bank%d" % index)

        def load_words(words, source):
            nc.sync.dma_start(out=words[:].bitcast(I32), in_=source.rearrange("p n t -> p (n t)").bitcast(I32))
            return words

        def load_table_scales(queue, tile, source, quadrants):
            for q in range(quadrants):
                queue.dma_start(
                    out=tile[32 * q : 32 * q + SCALE_ROWS * K_PASSES, :].bitcast(I32),
                    in_=source[:, SCALE_ROWS * q : SCALE_ROWS * (q + 1), :].bitcast(I32),
                )

        def part_of_list(b):
            return neigh_list[:, b * LIST_COLS : (b + 1) * LIST_COLS]

        def gather_centres(picked, window):
            nc.vector.tensor_copy(picked[:], window[:].indirect(centre_list[:]))
            return picked

        def gather_dealt(picked, window, b):
            nc.vector.tensor_copy(picked[:].rearrange("p t m -> p m t"), window[:].indirect(part_of_list(b)))
            return picked

        centre_list = lists.tile([P, S2 // 16], U16, name="centre_list")
        neigh_list = lists.tile([P, S // 16], U16, name="neigh_list")
        neigh_scales = tile_at(13 * KIB, "neigh_scales", [P, T], U8)
        centre_scales = tile_at(9 * KIB + 512, "centre_scales", [P, T2], U8)
        zeros = tile_in(early, "zeros", [P, P], F32)
        identity = tile_in(early, "identity", [P, P], F32)
        centre_words, neigh_words = {}, {}
        dealt = [P, PACK, P]

        def load_adj(rows, b):
            nc.sync.dma_start(out=rows[:], in_=adj[b * PASS : (b + 1) * PASS, :].rearrange("(p t) j -> p t j", t=PACK))
            return rows

        with tc.tile_pool(name="head", bufs=1) as head:
            nc.sync.dma_start(centre_list[:], offs2)
            centre_table = [load_words(tile_in(early, "centre_table0", [P, T2], U32), tab2_words[0])]
            centre_table.append(load_words(tile_at(31 * KIB, "centre_table1", [P, T2], U32), tab2_words[1]))
            nc.sync.dma_start(neigh_list[:], offs)
            neigh_table = [load_words(tile_in(head, "neigh_table0", [P, T], U32), tab_words[0])]
            centre_table.append(load_words(tile_at(0, "centre_table2", [P, T2], U32), tab2_words[2]))
            neigh_table.append(load_words(tile_in(early, "neigh_table1", [P, T], U32), tab_words[1]))

            nc.vector.memset(neigh_scales[:].bitcast(I32), 0)
            load_table_scales(nc.gpsimd, neigh_scales, tab_scales, QUADRANTS)
            nc.vector.memset(centre_scales[:].bitcast(I32), 0)
            load_table_scales(nc.scalar, centre_scales, tab2_scales, QUADRANTS)
            nc.vector.memset(zeros[:], 0.0)
            nc.gpsimd.affine_select(
                out=identity[:], in_=zeros[:], compare_op=NOT_EQUAL, fill=1.0, base=0, pattern=[[-1, P]], channel_multiplier=1
            )
            for a in (0, 1):
                centre_words[a] = gather_centres(tile_in(early, "centre_words%d" % a, [P, S2], U32), centre_table[a])

            deg_cols = tile_at(34 * KIB, "deg_cols", [P, I_PASSES, PACK], F32)
            nc.sync.dma_start(out=deg_cols[:], in_=deg.rearrange("(b p t) -> p b t", p=P, t=PACK))
            half_deg = tile_in(early, "half_deg", [P, I_PASSES, PACK], F32)
            nc.scalar.activation(half_deg[:], deg_cols[:], COPY, scale=0.5)
            neigh_table.append(load_words(tile_at(24 * KIB, "neigh_table2", [P, T], U32), tab_words[2]))
            adj_rows = [load_adj(tile_at(34 * KIB + 512, "adj0", [P, PACK, S2], F32), 0)]
            bias_rows = tile_at(33 * KIB + 512, "bias_rows", [P, P], F32)
            nc.vector.memset(bias_rows[:], 0.0)
            nc.sync.dma_start(out=bias_rows[0:N_TILES, :], in_=bg.rearrange("(n p) -> n p", p=P))
            msg_scales = tile_at(32 * KIB, "msg_scales", [P, I_PASSES * N], U8)
            nc.vector.memset(msg_scales[:].bitcast(I32), 0)
            for q in range(QUADRANTS):
                nc.sync.dma_start(
                    out=msg_scales[32 * q : 32 * q + SCALE_ROWS, :].rearrange("r (a n) -> r a n", a=I_PASSES).bitcast(I32),
                    in_=m4_scales[:, SCALE_ROWS * q : SCALE_ROWS * (q + 1), :].rearrange("a r n -> r a n").bitcast(I32),
                )
            for b in range(I_PASSES):
                neigh_words[(0, b)] = gather_dealt(tile_in(early, "neigh_words0_%d" % b, dealt, U32), neigh_table[0], b)

        rest = ctx.enter_context(tc.tile_pool(name="rest", bufs=1))

        places = {"free": 0}

        def sbuf(name, shape, dtype, over=None, shift=0):
            if over is None:
                places[name] = places["free"]
                places["free"] = places[name] + max(64, math.prod(shape[1:]) * BYTES_OF[dtype])
            else:
                places[name] = places[over] + shift
            return rest.tile(shape, dtype, name=name, tag=name, align_bytes=64, offset=places[name])

        wg_rows = {}
        piece = [P, PACK, W_CHUNK]

        def load_wg(b, c, rows):
            width = rows.shape[2]
            source = wg[b * PASS : (b + 1) * PASS, c * W_CHUNK : c * W_CHUNK + width]
            nc.sync.dma_start(out=rows[:], in_=source.rearrange("(p t) n -> p t n", t=PACK))
            for k in range(width // W_CHUNK):
                wg_rows[(b, c + k)] = rows[:, :, k * W_CHUNK : (k + 1) * W_CHUNK]

        msg_words = {}

        def load_messages(tiles, words):
            source = m4_words[:, :, 2 * P * tiles[0] : 2 * P * (tiles[-1] + 1)]
            nc.sync.dma_start(out=words[:].bitcast(I32), in_=source.rearrange("a p c -> p a c").bitcast(I32))
            for place, n in enumerate(tiles):
                msg_words[n] = words[:, :, 2 * P * place : 2 * P * (place + 1)]

        load_wg(0, 0, sbuf("wg0_0", [P, PACK, 2 * W_CHUNK], F32))
        adj_rows.append(load_adj(sbuf("adj1", [P, PACK, S2], F32), 1))
        load_wg(1, 0, sbuf("wg1_0", [P, PACK, 2 * W_CHUNK], F32))
        load_messages((0, 1, 2, 3), sbuf("first_messages", [P, I_PASSES, 8 * P], U8))

        centre_words[2] = gather_centres(tile_in(early, "centre_words2", [P, S2], U32), centre_table[2])
        centre_bytes = gather_centres(tile_at(0, "centre_bytes", [P, S2], U8), centre_scales)
        neigh_bytes = [
            gather_dealt(tile_at((b + 1) * PASS, "neigh_bytes%d" % b, dealt, U8), neigh_scales, b) for b in range(I_PASSES)
        ]
        neigh_words[(1, 0)] = gather_dealt(tile_at(8 * KIB, "neigh_words1_0", dealt, U32), neigh_table[1], 0)
        neigh_words[(2, 0)] = gather_dealt(tile_at(14 * KIB, "neigh_words2_0", dealt, U32), neigh_table[2], 0)
        neigh_words[(2, 1)] = gather_dealt(tile_at(2 * KIB, "neigh_words2_1", dealt, U32), neigh_table[2], 1)
        neigh_words[(1, 1)] = gather_dealt(tile_at(29 * KIB, "neigh_words1_1", dealt, U32), neigh_table[1], 1)

        compare = {(b, c): bank(b * J_CHUNKS + c, [P, PACK, J_CHUNK]) for b in range(I_PASSES) for c in range(J_CHUNKS)}
        steps = ((0, 0), (0, 1), (1, 0), (2, 0), (2, 1), (1, 1))
        for a, b in steps:
            last = [step for step in steps if step[1] == b][-1]
            for c in range(J_CHUNKS):
                cols = slice(c * J_CHUNK, (c + 1) * J_CHUNK)
                for t in range(PACK):
                    nc.tensor.matmul_mx(
                        out=compare[(b, c)][:, t, :],
                        lhsT=neigh_words[(a, b)][:, t, :].bitcast(FP8X4),
                        lhsT_scale=neigh_bytes[b][SCALE_ROWS * a :, t, :],
                        rhs=centre_words[a][:, cols].bitcast(FP8X4),
                        rhs_scale=centre_bytes[SCALE_ROWS * a :, cols],
                        start=(a == 0 and t == 0),
                        stop=((a, b) == last and t == PACK - 1),
                    )

        for b in range(I_PASSES):
            load_wg(b, 2, tile_at((23 + 4 * b) * KIB, "wg%d_2" % b, piece, F32))
        load_messages((4, 5), tile_at(31 * KIB, "last_messages", [P, I_PASSES, 4 * P], U8))

        def interleaved(tile, run):
            return tile.rearrange("p (r i) t -> p r t i", i=run)

        def by_rows(tile, run):
            return tile.rearrange("p t (r i) -> p r t i", i=run)

        half = S2 // 2
        weights = {}

        def weigh_edges(b):
            for u in range(2):
                weight = sbuf("edge_weight%d_%d" % (b, u), [P, PACK, half], F32)
                for t in range(PACK):
                    nc.scalar.activation(
                        weight[:, t, :], adj_rows[b][:, t, u * half : (u + 1) * half], COPY, scale=half_deg[:, b, t : t + 1]
                    )
                weights[(b, u)] = weight

        wg_bf16, wg_codes, wg_scales = {}, {}, {}

        def round_wg(copy, b, tiles, over=None, shift=0):
            c, first = divmod(tiles[0] * P, W_CHUNK)
            width = len(tiles) * P
            rounded = sbuf("wg_bf16_%d_%d" % (b, tiles[0]), [P, width, PACK], BF16, over, shift)
            copy(interleaved(rounded[:], 4), by_rows(wg_rows[(b, c)][:, :, first : first + width], 4))
            wg_bf16[(b, tiles)] = rounded

        def quantise_wg(b, tiles, over=None, shift=0):
            width = len(tiles) * P
            codes = sbuf("wg_codes%d_%d" % (b, tiles[0]), [P, width], U32)
            scales = sbuf("wg_scales%d_%d" % (b, tiles[0]), [P, width], U8, over, shift)
            nc.vector.quantize_mx(
                out=codes[:].bitcast(FP8X4), scales=scales[:], in_=wg_bf16[(b, tiles)][:].rearrange("p n t -> p (n t)")
            )
            for place, n in enumerate(tiles):
                wg_codes[(b, n)] = codes[:, place * P : (place + 1) * P]
                wg_scales[(b, n)] = scales[:, place * P : (place + 1) * P]

        h_codes = [sbuf("h_codes%d" % b, [P, S2], U32) for b in range(I_PASSES)]
        h_scales = [sbuf("h_scales%d" % b, [P, S2], U8) for b in range(I_PASSES)]
        h_bf16 = {}

        def multiply_h(b, c):
            rounded = sbuf("h_bf16_%d_%d" % (b, c), [P, J_CHUNK, PACK], BF16)
            u, first = divmod(c * J_CHUNK, half)
            weight = weights[(b, u)][:, :, first : first + J_CHUNK]
            nc.vector.tensor_tensor(interleaved(rounded[:], 2), by_rows(compare[(b, c)][:], 2), by_rows(weight, 2), MULT)
            h_bf16[(b, c)] = rounded

        def quantise_h(b, c):
            cols = slice(c * J_CHUNK, (c + 1) * J_CHUNK)
            nc.vector.quantize_mx(
                out=h_codes[b][:, cols].bitcast(FP8X4),
                scales=h_scales[b][:, cols],
                in_=h_bf16[(b, c)][:].rearrange("p j t -> p (j t)"),
            )

        def make_h(b, between):
            for c in range(J_CHUNKS):
                multiply_h(b, c)
                if c > 0:
                    quantise_h(b, c - 1)
            between()
            quantise_h(b, J_CHUNKS - 1)

        weigh_edges(0)
        round_wg(nc.scalar.copy, 0, (0, 1))
        round_wg(nc.scalar.copy, 0, (2, 3))
        make_h(0, lambda: quantise_wg(0, (0, 1), "edge_weight0_0"))
        quantise_wg(0, (2, 3), "h_bf16_0_2")
        bias_turned = bank(0, [P, P])
        nc.tensor.transpose(bias_turned[:], bias_rows[:], identity[:])
        weigh_edges(1)
        half_bias = sbuf("half_bias", [P, N_TILES], F32, "adj1")
        nc.scalar.activation(half_bias[:], bias_turned[:, 0:N_TILES], COPY, scale=0.5)
        round_wg(nc.scalar.copy, 1, (0, 1))
        make_h(1, lambda: quantise_wg(1, (0, 1)))

        def message_pass(n, b, cols=slice(0, S2)):
            nc.tensor.matmul_mx(
                out=y_acc[n][:, cols],
                lhsT=msg_words[n][:, b, :].bitcast(FP4X4),
                lhsT_scale=msg_scales[:, b * N + P * n : b * N + P * (n + 1)],
                rhs=h_codes[b][:, cols].bitcast(FP8X4),
                rhs_scale=h_scales[b][:, cols],
                start=(b == 0),
                stop=(b == I_PASSES - 1 and cols.stop == S2),
            )

        def gate_pass(n, b, cols=slice(0, S2)):
            nc.tensor.matmul_mx(
                out=g_acc[n][:, cols],
                lhsT=wg_codes[(b, n)].bitcast(FP8X4),
                lhsT_scale=wg_scales[(b, n)],
                rhs=h_codes[b][:, cols].bitcast(FP8X4),
                rhs_scale=h_scales[b][:, cols],
                start=(b == 0),
                stop=(b == I_PASSES - 1 and cols.stop == S2),
            )

        def make_gate(n, gate, cols=slice(0, S2)):
            nc.scalar.activation(gate, g_acc[n][:, cols], TANH, bias=half_bias[:, n : n + 1])

        def finish(n, gate, result, cols=slice(0, S2)):
            nc.vector.scalar_tensor_tensor(result, gate, 1.0, y_acc[n][:, cols], ADD, MULT)
            nc.sync.dma_start(out=out[n * P : (n + 1) * P, cols], in_=result)

        whole = [P, S2]
        pair = [P, 2, S2]
        g_acc = {0: bank(0, whole), 1: bank(1, whole), 2: bank(6, whole), 3: bank(7, whole)}
        y_acc = {0: bank(2, whole), 1: bank(3, whole), 2: bank(4, whole), 3: bank(5, whole)}
        for n in (0, 1):
            gate_pass(n, 0)
        for n in (0, 1, 2, 3):
            message_pass(n, 0)
        first_half, second_half = slice(0, half), slice(half, S2)
        for n in (0, 1, 2, 3):
            message_pass(n, 1, first_half)
        for cols in (first_half, second_half):
            for n in (0, 1):
                gate_pass(n, 1, cols)
        for n in (0, 1, 2, 3):
            message_pass(n, 1, second_half)
        round_wg(nc.scalar.copy, 1, (2, 3))
        quantise_wg(1, (2, 3), "h_bf16_1_2")
        for b in range(I_PASSES):
            for n in (2, 3):
                gate_pass(n, b)
        gates = sbuf("gates0", pair, F32, "wg1_0")
        results = sbuf("results0", pair, F32)
        for n in (0, 1):
            make_gate(n, gates[:, n, :])
            finish(n, gates[:, n, :], results[:, n, :])
        round_wg(nc.scalar.copy, 0, (4, 5))
        quantise_wg(0, (4, 5), "h_bf16_1_3")
        for n in (4, 5):
            round_wg(nc.vector.tensor_copy, 1, (n,), "wg_bf16_1_2", (n - 4) * KIB)
        for n in (4, 5):
            quantise_wg(1, (n,))
        y_acc[4] = bank(2, whole)
        for b in range(I_PASSES):
            message_pass(4, b)
        for n in (4, 5):
            g_acc[n] = bank(n - 4, whole)
        for b in range(I_PASSES):
            for n in (4, 5):
                gate_pass(n, b)
        gates = tile_at(23 * KIB, "gates1", pair, F32)
        results = tile_at(27 * KIB, "results1", pair, F32)
        for n in (2, 3):
            make_gate(n, gates[:, n - 2, :])
            finish(n, gates[:, n - 2, :], results[:, n - 2, :])
        y_acc[5] = bank(4, whole)
        for b in range(I_PASSES):
            message_pass(5, b)
        gates = sbuf("gates2", pair, F32)
        results = sbuf("results2", pair, F32)
        for n, cols in ((4, slice(0, S2)), (5, first_half), (5, second_half)):
            make_gate(n, gates[:, n - 4, cols], cols)
            finish(n, gates[:, n - 4, cols], results[:, n - 4, cols], cols)
